import numpy as np
import ml_dtypes


def mxq(x, axis, fmt="e4m3"):
    dtype, down = {"e4m3": (ml_dtypes.float8_e4m3fn, 7), "e5m2": (ml_dtypes.float8_e5m2, 14)}[fmt]
    v = np.moveaxis(np.asarray(x, np.float32).astype(ml_dtypes.bfloat16).astype(np.float64), axis, -1)
    blocks = v.reshape(v.shape[:-1] + (-1, 32))
    amax = np.abs(blocks).max(-1, keepdims=True)
    byte = np.maximum(np.where(amax > 0, np.frexp(amax)[1] - 1 + 127, 0) - down, 1)
    scale = np.exp2(byte - 127.0)
    codes = (blocks / scale).astype(np.float32).astype(dtype).astype(np.float64)
    return np.moveaxis((codes * scale).reshape(v.shape), -1, axis)


WIDE = False


def mx_kscale(k):
    if not WIDE:
        return np.ones(k)
    levels = np.array([10, -10, 5, -5, 0])
    if k % 512:
        return np.exp2(np.random.permutation(np.resize(levels, k // 32))).repeat(32)
    a = np.empty((k // 512, 16))
    for p in range(k // 512):
        a[p, :8] = np.random.permutation(np.resize(levels, 8))
        for g in range(8):
            far = levels[np.abs(levels - a[p, g]) >= 10]
            a[p, g + 8] = far[np.random.randint(len(far))]
    return np.exp2(a.ravel()).repeat(32)


def f64(x):
    return np.asarray(x).astype(np.float64)


def striped8(idx):
    return np.concatenate([v.reshape(-1, 16).T for v in idx]).astype(np.uint16)


def unstriped8(offs):
    return np.stack([offs[16 * g:16 * g + 16].T.reshape(-1) for g in range(8)]).astype(np.int64)


E2M1 = np.array([0.0, 0.5, 1.0, 1.5, 2.0, 3.0, 4.0, 6.0, -0.0, -0.5, -1.0, -1.5, -2.0, -3.0, -4.0, -6.0])


def pack_weight(w, fmt):
    k, n = w.shape
    w = f64(np.asarray(w, np.float32).astype(ml_dtypes.bfloat16)).reshape(k // 32, 32, n)
    amax = np.abs(w).max(1)
    if fmt == "e4m3":
        byte = np.frexp(amax)[1] - 1 + 127 - 7
    else:
        mant, ex = np.frexp(amax / 6.0)
        byte = np.where(mant > 0.5, ex, ex - 1) + 127
    byte = np.clip(np.where(amax > 0, byte, 1), 1, 254)
    scaled = (w * np.exp2(127.0 - byte)[:, None, :]).reshape(k, n).astype(np.float32)
    by_word = np.ascontiguousarray(scaled.reshape(k // 512, 128, 4, n).transpose(0, 1, 3, 2))
    if fmt == "e4m3":
        words = by_word.astype(ml_dtypes.float8_e4m3fn).view(np.uint8)
    else:
        c = by_word.astype(ml_dtypes.float4_e2m1fn).view(np.uint8) & 0xF
        words = (c[..., 0::2] | (c[..., 1::2] << 4)).reshape(k // 512, 128, 2 * n)
    return np.ascontiguousarray(words), np.ascontiguousarray(byte.astype(np.uint8).reshape(k // 512, 16, n))


def unpack_weight(words, scales, fmt):
    g, _, n = scales.shape
    words = np.ascontiguousarray(words).reshape(g, 128, n, -1)
    if fmt == "e4m3":
        vals = words.view(ml_dtypes.float8_e4m3fn).astype(np.float64)
    else:
        nib = np.empty((g, 128, n, 4), np.uint8)
        nib[..., 0::2] = words & 0xF
        nib[..., 1::2] = words >> 4
        vals = E2M1[nib]
    vals = vals * np.repeat(np.exp2(scales.astype(np.float64) - 127.0), 8, axis=1)[..., None]
    return vals.transpose(0, 1, 3, 2).reshape(g * 512, n)


K, M, T, S = 1536, 1024, 512, 256


def setup_inputs():
    n = np.random.standard_normal
    s = mx_kscale(K)[:, None]
    u = mx_kscale(512)[:, None]
    p_w4 = pack_weight(n((K, M)) / np.sqrt(K) / s, "e2m1")
    return {
        "x": (n((K, S)) * s).astype(np.float32),
        "w4_words": p_w4[0],
        "w4_scales": p_w4[1],
        "down": (n((K, 512)) / np.sqrt(K) / s * u.T).astype(np.float32),
        "up": (0.5 * n((512, M)) / np.sqrt(512) / u).astype(np.float32),
        "wgo": np.repeat(np.random.uniform(0.5, 2.0, (8, S)), 16, axis=0).astype(np.float32),
        "offs": striped8(np.stack([np.random.permutation(T)[:S] for _ in range(8)])),
    }


def reference(x, w4_words, w4_scales, down, up, wgo, offs):
    x_ = mxq(f64(x), 0, "e4m3")
    w4_ = unpack_weight(w4_words, w4_scales, "e2m1")
    down_ = mxq(f64(down), 0, "e4m3")
    up_ = mxq(f64(up), 0, "e4m3")
    h_ = mxq(down_.T @ x_, 0, "e4m3")
    y = w4_.T @ x_ + up_.T @ h_
    place = unstriped8(offs)[np.arange(M) % 128 // 16]
    out = np.zeros((M, T))
    out[np.arange(M)[:, None], place] = f64(wgo)[np.arange(M) % 128] * (y)
    return out

@@ -1,0 +1,194 @@
+from contextlib import ExitStack
+
+import concourse.mybir as mybir
+
+K, M, T, S, R = 1536, 1024, 512, 256, 512
+FLOPS = 2 * S * (K * R + K * M + R * M)
+
+F32 = mybir.dt.float32
+BF16 = mybir.dt.bfloat16
+I32 = mybir.dt.int32
+U32 = mybir.dt.uint32
+U16 = mybir.dt.uint16
+U8 = mybir.dt.uint8
+FP8X4 = mybir.dt.float8_e4m3fn_x4
+FP4X4 = mybir.dt.float4_e2m1fn_x4
+
+P = 128
+PACK = 4
+K_PASS = P * PACK
+PASSES = K // K_PASS
+HALF = 128
+HALVES = S // HALF
+ROW_TILES = M // P
+PAIR = 2 * P
+
+
+def tile_list_hscat_l_none_kernel(tc, x, w4_words, w4_scales, down, up, wgo, offs, out):
+    nc = tc.nc
+    with ExitStack() as ctx:
+        keep = ctx.enter_context(tc.tile_pool(name="keep", bufs=1))
+        stage = ctx.enter_context(tc.tile_pool(name="stage", bufs=4))
+        h_psum = ctx.enter_context(tc.psum_pool(name="h_psum", bufs=1))
+        y_psum = ctx.enter_context(tc.psum_pool(name="y_psum", bufs=6))
+
+        offsets = keep.tile([P, S // 16], U16, name="offsets")
+
+        w4_ranges = [(0, 2), (2, ROW_TILES)]
+        w4_code = [keep.tile([P, PASSES, 2 * P * (hi - lo)], U8, name="w4_code%d" % lo, align_bytes=64) for lo, hi in w4_ranges]
+        w4_scale = [keep.tile([P, PASSES, P * (hi - lo)], U8, name="w4_scale%d" % lo, align_bytes=64) for lo, hi in w4_ranges]
+        windows = [keep.tile([P, T], F32, name="window%d" % n) for n in range(ROW_TILES)]
+        for plane in w4_scale:
+            nc.vector.memset(plane[:].rearrange("p a n -> p (a n)").bitcast(U32), 0)
+        for window in windows:
+            nc.vector.memset(window[:], 0.0)
+
+        def load_rows(rows, name):
+            raw = keep.tile([P, PACK, rows.shape[1]], F32, name=name)
+            nc.sync.dma_start(out=raw[:], in_=rows.rearrange("(p i) c -> p i c", i=PACK))
+            return raw
+
+        def load_w4(c):
+            lo, hi = w4_ranges[c]
+            for q in range(4):
+                nc.sync.dma_start(
+                    out=w4_scale[c][32 * q : 32 * q + 4, :, :].bitcast(I32),
+                    in_=w4_scales[:, 4 * q : 4 * q + 4, P * lo : P * hi].rearrange("a r n -> r a n").bitcast(I32),
+                )
+            nc.sync.dma_start(
+                out=w4_code[c][:].bitcast(I32),
+                in_=w4_words[:, :, 2 * P * lo : 2 * P * hi].rearrange("a p n -> p a n").bitcast(I32),
+            )
+
+        down_raw = []
+        for a in range(PASSES):
+            down_raw.append(load_rows(down[a * K_PASS : (a + 1) * K_PASS, :], "down_raw%d" % a))
+            if a == 0:
+                nc.sync.dma_start(offsets[:], offs)
+        x_raw = [load_rows(x[a * K_PASS : (a + 1) * K_PASS, :], "x_raw%d" % a) for a in range(PASSES)]
+        up_raw = [load_rows(up[:, 0:PAIR], "up_raw0")]
+        load_w4(0)
+        weights = keep.tile([P, S], F32, name="weights")
+        nc.sync.dma_start(out=weights[:], in_=wgo)
+        up_raw.append(load_rows(up[:, PAIR : 2 * PAIR], "up_raw1"))
+        load_w4(1)
+        for u in range(2, ROW_TILES // 2):
+            up_raw.append(load_rows(up[:, u * PAIR : (u + 1) * PAIR], "up_raw%d" % u))
+
+        def cast(on_vector, dst, src):
+            if on_vector:
+                nc.vector.tensor_copy(out=dst, in_=src)
+            else:
+                nc.scalar.copy(out=dst, in_=src)
+
+        def interleave(on_vector, raw_cols, name):
+            width = raw_cols.shape[2]
+            grouped = keep.tile([P, width, PACK], BF16, name=name, align_bytes=64)
+            cast(
+                on_vector,
+                grouped[:].rearrange("p (c e) i -> p c i e", e=4),
+                raw_cols.rearrange("p i (c e) -> p c i e", e=4),
+            )
+            return grouped[:].rearrange("p c i -> p (c i)")
+
+        def quantize(flat, name):
+            width = flat.shape[1] // PACK
+            codes = keep.tile([P, width], U32, name=name + "_codes", align_bytes=64)
+            scales = keep.tile([P, width], U8, name=name + "_scales", align_bytes=64)
+            nc.vector.quantize_mx(out=codes[:].bitcast(FP8X4), scales=scales[:], in_=flat)
+            return codes, scales
+
+        down_q = {}
+        for a in range(PASSES):
+            flats = {}
+            for tp in (1, 0):
+                grouped = keep.tile([P, 2, P, PACK], BF16, name="down_bf%d_%d" % (a, tp), align_bytes=64)
+                cast(
+                    tp == 1,
+                    grouped[:].rearrange("p t m i -> p m i t"),
+                    down_raw[a][:].rearrange("p i (m t) -> p m i t", t=PACK)[:, :, :, 2 * tp : 2 * tp + 2],
+                )
+                flats[tp] = grouped[:].rearrange("p t m i -> p (t m i)")
+            for tp in (1, 0):
+                down_q[a, tp] = quantize(flats[tp], "down%d_%d" % (a, tp))
+
+        h_acc = [h_psum.tile([P, PACK, HALF], F32, name="h_acc%d" % half) for half in range(HALVES)]
+        x_q = {}
+        for a in range(PASSES):
+            flats = [
+                interleave(half == 0, x_raw[a][:, :, half * HALF : (half + 1) * HALF], "x_bf%d_%d" % (a, half))
+                for half in range(HALVES)
+            ]
+            for half in range(HALVES):
+                x_q[a, half] = quantize(flats[half], "x%d_%d" % (a, half))
+                x_codes, x_scales = x_q[a, half]
+                for t in range(PACK):
+                    d_codes, d_scales = down_q[a, t // 2]
+                    cols = slice((t % 2) * P, (t % 2 + 1) * P)
+                    nc.tensor.matmul_mx(
+                        out=h_acc[half][:, t, :],
+                        lhsT=d_codes[:, cols].bitcast(FP8X4),
+                        lhsT_scale=d_scales[:, cols],
+                        rhs=x_codes[:].bitcast(FP8X4),
+                        rhs_scale=x_scales[:],
+                        start=(a == 0 and t == 0),
+                        stop=(a == PASSES - 1 and t == PACK - 1),
+                    )
+
+        def quantize_h(half):
+            grouped = keep.tile([P, HALF, PACK], BF16, name="h_bf%d" % half, align_bytes=64)
+            nc.scalar.copy(out=grouped[:], in_=h_acc[half][:].rearrange("p t j -> p j t"))
+            return quantize(grouped[:].rearrange("p j t -> p (j t)"), "h%d" % half)
+
+        def up_tile(n, on_vector):
+            return interleave(on_vector, up_raw[n // 2][:, :, (n % 2) * P : (n % 2 + 1) * P], "up_bf%d" % n)
+
+        h_q = {}
+        up_q = {}
+        h_q[0] = quantize_h(0)
+        up_q[0] = quantize(up_tile(0, True), "up0")
+        up_q[1] = quantize(up_tile(1, True), "up1")
+        h_q[1] = quantize_h(1)
+
+        def product(n, half):
+            c = 0 if n < w4_ranges[0][1] else 1
+            col = n - w4_ranges[c][0]
+            acc = y_psum.tile([P, HALF], F32, name="y_acc")
+            for a in range(PASSES):
+                x_codes, x_scales = x_q[a, half]
+                nc.tensor.matmul_mx(
+                    out=acc[:],
+                    lhsT=w4_code[c][:, a, 2 * P * col : 2 * P * (col + 1)].bitcast(FP4X4),
+                    lhsT_scale=w4_scale[c][:, a, P * col : P * (col + 1)],
+                    rhs=x_codes[:].bitcast(FP8X4),
+                    rhs_scale=x_scales[:],
+                    start=(a == 0),
+                    stop=False,
+                )
+            nc.tensor.matmul_mx(
+                out=acc[:],
+                lhsT=up_q[n][0][:].bitcast(FP8X4),
+                lhsT_scale=up_q[n][1][:],
+                rhs=h_q[half][0][:].bitcast(FP8X4),
+                rhs_scale=h_q[half][1][:],
+                start=False,
+                stop=True,
+            )
+            y = stage.tile([P, HALF], F32, name="y")
+            nc.scalar.copy(out=y[:], in_=acc[:])
+            nc.vector.tensor_tensor(
+                windows[n][:].indirect(offsets[:, half * (HALF // 16) : (half + 1) * (HALF // 16)]),
+                y[:],
+                weights[:, half * HALF : (half + 1) * HALF],
+                mybir.AluOpType.mult,
+            )
+
+        for u in range(ROW_TILES // 2):
+            for half in range(HALVES):
+                for n in (2 * u, 2 * u + 1):
+                    product(n, half)
+                    if half == HALVES - 1:
+                        nc.sync.dma_start(out=out[n * P : (n + 1) * P, :], in_=windows[n][:])
+                if half == 0 and 2 * u + 2 < ROW_TILES:
+                    for n in (2 * u + 2, 2 * u + 3):
+                        up_q[n] = quantize(up_tile(n, False), "up%d" % n)

@@ -28,15 +28,15 @@ def tile_list_hscat_l_none_kernel(tc, x, w4_words, w4_scales, down, up, wgo, off
     nc = tc.nc
     with ExitStack() as ctx:
         keep = ctx.enter_context(tc.tile_pool(name="keep", bufs=1))
-        stage = ctx.enter_context(tc.tile_pool(name="stage", bufs=4))
         h_psum = ctx.enter_context(tc.psum_pool(name="h_psum", bufs=1))
         y_psum = ctx.enter_context(tc.psum_pool(name="y_psum", bufs=6))
 
         offsets = keep.tile([P, S // 16], U16, name="offsets")
 
-        w4_ranges = [(0, 2), (2, ROW_TILES)]
+        w4_ranges = [(0, 2), (2, 4), (4, ROW_TILES)]
+        scale_ranges = [(0, 2), (2, ROW_TILES)]
         w4_code = [keep.tile([P, PASSES, 2 * P * (hi - lo)], U8, name="w4_code%d" % lo, align_bytes=64) for lo, hi in w4_ranges]
-        w4_scale = [keep.tile([P, PASSES, P * (hi - lo)], U8, name="w4_scale%d" % lo, align_bytes=64) for lo, hi in w4_ranges]
+        w4_scale = [keep.tile([P, PASSES, P * (hi - lo)], U8, name="w4_scale%d" % lo, align_bytes=64) for lo, hi in scale_ranges]
         windows = [keep.tile([P, T], F32, name="window%d" % n) for n in range(ROW_TILES)]
         for plane in w4_scale:
             nc.vector.memset(plane[:].rearrange("p a n -> p (a n)").bitcast(U32), 0)
@@ -48,13 +48,16 @@ def tile_list_hscat_l_none_kernel(tc, x, w4_words, w4_scales, down, up, wgo, off
             nc.sync.dma_start(out=raw[:], in_=rows.rearrange("(p i) c -> p i c", i=PACK))
             return raw
 
-        def load_w4(c):
-            lo, hi = w4_ranges[c]
+        def load_scales(c):
+            lo, hi = scale_ranges[c]
             for q in range(4):
                 nc.sync.dma_start(
                     out=w4_scale[c][32 * q : 32 * q + 4, :, :].bitcast(I32),
                     in_=w4_scales[:, 4 * q : 4 * q + 4, P * lo : P * hi].rearrange("a r n -> r a n").bitcast(I32),
                 )
+
+        def load_codes(c):
+            lo, hi = w4_ranges[c]
             nc.sync.dma_start(
                 out=w4_code[c][:].bitcast(I32),
                 in_=w4_words[:, :, 2 * P * lo : 2 * P * hi].rearrange("a p n -> p a n").bitcast(I32),
@@ -67,13 +70,15 @@ def tile_list_hscat_l_none_kernel(tc, x, w4_words, w4_scales, down, up, wgo, off
                 nc.sync.dma_start(offsets[:], offs)
         x_raw = [load_rows(x[a * K_PASS : (a + 1) * K_PASS, :], "x_raw%d" % a) for a in range(PASSES)]
         up_raw = [load_rows(up[:, 0:PAIR], "up_raw0")]
-        load_w4(0)
+        load_scales(0)
+        load_codes(0)
         weights = keep.tile([P, S], F32, name="weights")
         nc.sync.dma_start(out=weights[:], in_=wgo)
         up_raw.append(load_rows(up[:, PAIR : 2 * PAIR], "up_raw1"))
-        load_w4(1)
+        load_scales(1)
         for u in range(2, ROW_TILES // 2):
             up_raw.append(load_rows(up[:, u * PAIR : (u + 1) * PAIR], "up_raw%d" % u))
+            load_codes(u - 1)
 
         def cast(on_vector, dst, src):
             if on_vector:
@@ -135,60 +140,74 @@ def tile_list_hscat_l_none_kernel(tc, x, w4_words, w4_scales, down, up, wgo, off
                         stop=(a == PASSES - 1 and t == PACK - 1),
                     )
 
+        h_codes = keep.tile([P, S], U32, name="h_codes", align_bytes=64)
+        h_scales = keep.tile([P, S], U8, name="h_scales", align_bytes=64)
+
         def quantize_h(half):
             grouped = keep.tile([P, HALF, PACK], BF16, name="h_bf%d" % half, align_bytes=64)
             nc.scalar.copy(out=grouped[:], in_=h_acc[half][:].rearrange("p t j -> p j t"))
-            return quantize(grouped[:].rearrange("p j t -> p (j t)"), "h%d" % half)
+            cols = slice(half * HALF, (half + 1) * HALF)
+            nc.vector.quantize_mx(
+                out=h_codes[:, cols].bitcast(FP8X4), scales=h_scales[:, cols], in_=grouped[:].rearrange("p j t -> p (j t)")
+            )
 
         def up_tile(n, on_vector):
             return interleave(on_vector, up_raw[n // 2][:, :, (n % 2) * P : (n % 2 + 1) * P], "up_bf%d" % n)
 
-        h_q = {}
         up_q = {}
-        h_q[0] = quantize_h(0)
+        quantize_h(0)
         up_q[0] = quantize(up_tile(0, True), "up0")
         up_q[1] = quantize(up_tile(1, True), "up1")
-        h_q[1] = quantize_h(1)
+        quantize_h(1)
 
-        def product(n, half):
-            c = 0 if n < w4_ranges[0][1] else 1
+        def product(n, halves):
+            c = max(i for i, (lo, hi) in enumerate(w4_ranges) if lo <= n)
             col = n - w4_ranges[c][0]
-            acc = y_psum.tile([P, HALF], F32, name="y_acc")
+            d = max(i for i, (lo, hi) in enumerate(scale_ranges) if lo <= n)
+            scol = n - scale_ranges[d][0]
+            width = HALF * len(halves)
+            cols = slice(halves[0] * HALF, halves[0] * HALF + width)
+            acc = y_psum.tile([P, width], F32, name="y_acc")
             for a in range(PASSES):
-                x_codes, x_scales = x_q[a, half]
-                nc.tensor.matmul_mx(
-                    out=acc[:],
-                    lhsT=w4_code[c][:, a, 2 * P * col : 2 * P * (col + 1)].bitcast(FP4X4),
-                    lhsT_scale=w4_scale[c][:, a, P * col : P * (col + 1)],
-                    rhs=x_codes[:].bitcast(FP8X4),
-                    rhs_scale=x_scales[:],
-                    start=(a == 0),
-                    stop=False,
-                )
+                for i, half in enumerate(halves):
+                    x_codes, x_scales = x_q[a, half]
+                    nc.tensor.matmul_mx(
+                        out=acc[:, i * HALF : (i + 1) * HALF],
+                        lhsT=w4_code[c][:, a, 2 * P * col : 2 * P * (col + 1)].bitcast(FP4X4),
+                        lhsT_scale=w4_scale[d][:, a, P * scol : P * (scol + 1)],
+                        rhs=x_codes[:].bitcast(FP8X4),
+                        rhs_scale=x_scales[:],
+                        start=(a == 0 and i == 0),
+                        stop=False,
+                    )
             nc.tensor.matmul_mx(
                 out=acc[:],
                 lhsT=up_q[n][0][:].bitcast(FP8X4),
                 lhsT_scale=up_q[n][1][:],
-                rhs=h_q[half][0][:].bitcast(FP8X4),
-                rhs_scale=h_q[half][1][:],
+                rhs=h_codes[:, cols].bitcast(FP8X4),
+                rhs_scale=h_scales[:, cols],
                 start=False,
                 stop=True,
             )
-            y = stage.tile([P, HALF], F32, name="y")
+            y = keep.tile([P, width], F32, name="y%d_%d" % (n, halves[0]))
             nc.scalar.copy(out=y[:], in_=acc[:])
             nc.vector.tensor_tensor(
-                windows[n][:].indirect(offsets[:, half * (HALF // 16) : (half + 1) * (HALF // 16)]),
+                windows[n][:].indirect(offsets[:, cols.start // 16 : cols.stop // 16]),
                 y[:],
-                weights[:, half * HALF : (half + 1) * HALF],
+                weights[:, cols],
                 mybir.AluOpType.mult,
             )
 
-        for u in range(ROW_TILES // 2):
-            for half in range(HALVES):
-                for n in (2 * u, 2 * u + 1):
-                    product(n, half)
-                    if half == HALVES - 1:
-                        nc.sync.dma_start(out=out[n * P : (n + 1) * P, :], in_=windows[n][:])
-                if half == 0 and 2 * u + 2 < ROW_TILES:
-                    for n in (2 * u + 2, 2 * u + 3):
-                        up_q[n] = quantize(up_tile(n, False), "up%d" % n)
+        def store(n):
+            nc.sync.dma_start(out=out[n * P : (n + 1) * P, :], in_=windows[n][:])
+
+        for half in range(HALVES):
+            for n in (0, 1):
+                product(n, [half])
+                if half == HALVES - 1:
+                    store(n)
+        for n in range(2, ROW_TILES):
+            up_q[n] = quantize(up_tile(n, False), "up%d" % n)
+        for n in range(2, ROW_TILES):
+            product(n, [0, 1])
+            store(n)

@@ -21,7 +21,15 @@ PASSES = K // K_PASS
 HALF = 128
 HALVES = S // HALF
 ROW_TILES = M // P
-PAIR = 2 * P
+
+LOADS = [('down', 0), ('offs',), ('down', 1), ('down', 2), ('x', 0, 0, 2), ('x', 1, 0, 2), ('x', 2, 0, 2), ('up', 0, 2), ('w', 0, 2), ('sc', 0, 4), ('up', 2, 3), ('wgo',), ('up', 3, 4), ('w', 2, 4), ('up', 4, 6), ('sc', 4, 8), ('w', 4, 8), ('up', 6, 8)]
+POOL_MEMSETS = []
+X_ON_V = [(0, 0), (1, 0), (2, 0)]
+H_ON_V = []
+UP_ON_V = [0, 1, 2]
+Y_ON_V = []
+TIES = {}
+STEPS = [('qd', 0), ('qd', 1), ('qd', 2), ('qx', 0, 0), ('h', 0, 0), ('qx', 1, 0), ('h', 1, 0), ('qx', 2, 0), ('h', 2, 0), ('qh', 0), ('qu', 0), ('y', 0, 0, 1), ('qx', 0, 1), ('h', 0, 1), ('qx', 1, 1), ('h', 1, 1), ('qx', 2, 1), ('h', 2, 1), ('qu', 1), ('qh', 1), ('y', 1, 0, 1), ('y', 0, 1, 2), ('qu', 2), ('y', 1, 1, 2), ('qu', 3), ('y', 2, 0, 2), ('qu', 4), ('y', 3, 0, 2), ('qu', 5), ('y', 4, 0, 2), ('qu', 6), ('y', 5, 0, 2), ('qu', 7), ('y', 6, 0, 2), ('y', 7, 0, 2)]
 
 
 def tile_list_hscat_l_none_kernel(tc, x, w4_words, w4_scales, down, up, wgo, offs, out):
@@ -32,53 +40,61 @@ def tile_list_hscat_l_none_kernel(tc, x, w4_words, w4_scales, down, up, wgo, off
         y_psum = ctx.enter_context(tc.psum_pool(name="y_psum", bufs=6))
 
         offsets = keep.tile([P, S // 16], U16, name="offsets")
-
-        w4_ranges = [(0, 2), (2, 4), (4, ROW_TILES)]
-        scale_ranges = [(0, 2), (2, ROW_TILES)]
-        w4_code = [keep.tile([P, PASSES, 2 * P * (hi - lo)], U8, name="w4_code%d" % lo, align_bytes=64) for lo, hi in w4_ranges]
-        w4_scale = [keep.tile([P, PASSES, P * (hi - lo)], U8, name="w4_scale%d" % lo, align_bytes=64) for lo, hi in scale_ranges]
+        weights = keep.tile([P, S], F32, name="weights")
         windows = [keep.tile([P, T], F32, name="window%d" % n) for n in range(ROW_TILES)]
-        for plane in w4_scale:
-            nc.vector.memset(plane[:].rearrange("p a n -> p (a n)").bitcast(U32), 0)
-        for window in windows:
-            nc.vector.memset(window[:], 0.0)
+        scale_tile = {}
+        for item in LOADS:
+            if item[0] == "sc":
+                lo, hi = item[1:]
+                plane = keep.tile([P, PASSES, P * (hi - lo)], U8, name="w4_scale%d" % lo, align_bytes=64)
+                nc.vector.memset(plane[:].rearrange("p a n -> p (a n)").bitcast(U32), 0)
+                scale_tile[lo] = plane
+        for n, window in enumerate(windows):
+            (nc.gpsimd if n in POOL_MEMSETS else nc.vector).memset(window[:], 0.0)
 
         def load_rows(rows, name):
-            raw = keep.tile([P, PACK, rows.shape[1]], F32, name=name)
+            raw = keep.tile([P, PACK, rows.shape[1]], F32, name=name, tag=name)
             nc.sync.dma_start(out=raw[:], in_=rows.rearrange("(p i) c -> p i c", i=PACK))
             return raw
 
-        def load_scales(c):
-            lo, hi = scale_ranges[c]
-            for q in range(4):
-                nc.sync.dma_start(
-                    out=w4_scale[c][32 * q : 32 * q + 4, :, :].bitcast(I32),
-                    in_=w4_scales[:, 4 * q : 4 * q + 4, P * lo : P * hi].rearrange("a r n -> r a n").bitcast(I32),
-                )
-
-        def load_codes(c):
-            lo, hi = w4_ranges[c]
-            nc.sync.dma_start(
-                out=w4_code[c][:].bitcast(I32),
-                in_=w4_words[:, :, 2 * P * lo : 2 * P * hi].rearrange("a p n -> p a n").bitcast(I32),
-            )
-
-        down_raw = []
-        for a in range(PASSES):
-            down_raw.append(load_rows(down[a * K_PASS : (a + 1) * K_PASS, :], "down_raw%d" % a))
-            if a == 0:
+        down_raw, x_raw, up_raw, w4_code, w4_scale = {}, {}, {}, {}, {}
+        for item in LOADS:
+            kind = item[0]
+            if kind == "offs":
                 nc.sync.dma_start(offsets[:], offs)
-        x_raw = [load_rows(x[a * K_PASS : (a + 1) * K_PASS, :], "x_raw%d" % a) for a in range(PASSES)]
-        up_raw = [load_rows(up[:, 0:PAIR], "up_raw0")]
-        load_scales(0)
-        load_codes(0)
-        weights = keep.tile([P, S], F32, name="weights")
-        nc.sync.dma_start(out=weights[:], in_=wgo)
-        up_raw.append(load_rows(up[:, PAIR : 2 * PAIR], "up_raw1"))
-        load_scales(1)
-        for u in range(2, ROW_TILES // 2):
-            up_raw.append(load_rows(up[:, u * PAIR : (u + 1) * PAIR], "up_raw%d" % u))
-            load_codes(u - 1)
+            elif kind == "wgo":
+                nc.sync.dma_start(out=weights[:], in_=wgo)
+            elif kind == "down":
+                a = item[1]
+                down_raw[a] = load_rows(down[a * K_PASS : (a + 1) * K_PASS, :], "down_raw%d" % a)
+            elif kind == "x":
+                a, lo, hi = item[1:]
+                raw = load_rows(x[a * K_PASS : (a + 1) * K_PASS, lo * HALF : hi * HALF], "x_raw%d_%d" % (a, lo))
+                for half in range(lo, hi):
+                    x_raw[a, half] = raw[:, :, (half - lo) * HALF : (half - lo + 1) * HALF]
+            elif kind == "up":
+                lo, hi = item[1:]
+                raw = load_rows(up[:, lo * P : hi * P], "up_raw%d" % lo)
+                for n in range(lo, hi):
+                    up_raw[n] = raw[:, :, (n - lo) * P : (n - lo + 1) * P]
+            elif kind == "sc":
+                lo, hi = item[1:]
+                for q in range(4):
+                    nc.sync.dma_start(
+                        out=scale_tile[lo][32 * q : 32 * q + 4, :, :].bitcast(I32),
+                        in_=w4_scales[:, 4 * q : 4 * q + 4, P * lo : P * hi].rearrange("a r n -> r a n").bitcast(I32),
+                    )
+                for n in range(lo, hi):
+                    w4_scale[n] = scale_tile[lo][:, :, (n - lo) * P : (n - lo + 1) * P]
+            else:
+                lo, hi = item[1:]
+                codes = keep.tile([P, PASSES, 2 * P * (hi - lo)], U8, name="w4_code%d" % lo, align_bytes=64)
+                nc.sync.dma_start(
+                    out=codes[:].bitcast(I32),
+                    in_=w4_words[:, :, 2 * P * lo : 2 * P * hi].rearrange("a p n -> p a n").bitcast(I32),
+                )
+                for n in range(lo, hi):
+                    w4_code[n] = codes[:, :, (n - lo) * 2 * P : (n - lo + 1) * 2 * P]
 
         def cast(on_vector, dst, src):
             if on_vector:
@@ -88,7 +104,7 @@ def tile_list_hscat_l_none_kernel(tc, x, w4_words, w4_scales, down, up, wgo, off
 
         def interleave(on_vector, raw_cols, name):
             width = raw_cols.shape[2]
-            grouped = keep.tile([P, width, PACK], BF16, name=name, align_bytes=64)
+            grouped = keep.tile([P, width, PACK], BF16, name=name, tag=name, align_bytes=64)
             cast(
                 on_vector,
                 grouped[:].rearrange("p (c e) i -> p c i e", e=4),
@@ -103,8 +119,12 @@ def tile_list_hscat_l_none_kernel(tc, x, w4_words, w4_scales, down, up, wgo, off
             nc.vector.quantize_mx(out=codes[:].bitcast(FP8X4), scales=scales[:], in_=flat)
             return codes, scales
 
-        down_q = {}
-        for a in range(PASSES):
+        down_q, x_q, up_q = {}, {}, {}
+        h_acc = [h_psum.tile([P, PACK, HALF], F32, name="h_acc%d" % half) for half in range(HALVES)]
+        h_codes = keep.tile([P, S], U32, name="h_codes", align_bytes=64)
+        h_scales = keep.tile([P, S], U8, name="h_scales", align_bytes=64)
+
+        def quantize_down(a):
             flats = {}
             for tp in (1, 0):
                 grouped = keep.tile([P, 2, P, PACK], BF16, name="down_bf%d_%d" % (a, tp), align_bytes=64)
@@ -117,67 +137,63 @@ def tile_list_hscat_l_none_kernel(tc, x, w4_words, w4_scales, down, up, wgo, off
             for tp in (1, 0):
                 down_q[a, tp] = quantize(flats[tp], "down%d_%d" % (a, tp))
 
-        h_acc = [h_psum.tile([P, PACK, HALF], F32, name="h_acc%d" % half) for half in range(HALVES)]
-        x_q = {}
-        for a in range(PASSES):
-            flats = [
-                interleave(half == 0, x_raw[a][:, :, half * HALF : (half + 1) * HALF], "x_bf%d_%d" % (a, half))
-                for half in range(HALVES)
-            ]
-            for half in range(HALVES):
-                x_q[a, half] = quantize(flats[half], "x%d_%d" % (a, half))
-                x_codes, x_scales = x_q[a, half]
-                for t in range(PACK):
-                    d_codes, d_scales = down_q[a, t // 2]
-                    cols = slice((t % 2) * P, (t % 2 + 1) * P)
-                    nc.tensor.matmul_mx(
-                        out=h_acc[half][:, t, :],
-                        lhsT=d_codes[:, cols].bitcast(FP8X4),
-                        lhsT_scale=d_scales[:, cols],
-                        rhs=x_codes[:].bitcast(FP8X4),
-                        rhs_scale=x_scales[:],
-                        start=(a == 0 and t == 0),
-                        stop=(a == PASSES - 1 and t == PACK - 1),
-                    )
+        def quantize_x(a, half):
+            x_q[a, half] = quantize(interleave((a, half) in X_ON_V, x_raw[a, half], "x_bf%d_%d" % (a, half)), "x%d_%d" % (a, half))
 
-        h_codes = keep.tile([P, S], U32, name="h_codes", align_bytes=64)
-        h_scales = keep.tile([P, S], U8, name="h_scales", align_bytes=64)
+        def h_pass(a, half):
+            x_codes, x_scales = x_q[a, half]
+            for t in range(PACK):
+                d_codes, d_scales = down_q[a, t // 2]
+                cols = slice((t % 2) * P, (t % 2 + 1) * P)
+                nc.tensor.matmul_mx(
+                    out=h_acc[half][:, t, :],
+                    lhsT=d_codes[:, cols].bitcast(FP8X4),
+                    lhsT_scale=d_scales[:, cols],
+                    rhs=x_codes[:].bitcast(FP8X4),
+                    rhs_scale=x_scales[:],
+                    start=(a == 0 and t == 0),
+                    stop=(a == PASSES - 1 and t == PACK - 1),
+                )
+
+        def warm(a, tp, count):
+            codes, scales = down_q[a, tp]
+            for i in range(count):
+                acc = y_psum.tile([P, 2 * P], F32, name="y_acc")
+                nc.tensor.matmul_mx(
+                    out=acc[:],
+                    lhsT=codes[:, 0:P].bitcast(FP8X4),
+                    lhsT_scale=scales[:, 0:P],
+                    rhs=codes[:].bitcast(FP8X4),
+                    rhs_scale=scales[:],
+                    start=True,
+                    stop=True,
+                )
 
         def quantize_h(half):
             grouped = keep.tile([P, HALF, PACK], BF16, name="h_bf%d" % half, align_bytes=64)
-            nc.scalar.copy(out=grouped[:], in_=h_acc[half][:].rearrange("p t j -> p j t"))
+            cast(half in H_ON_V, grouped[:], h_acc[half][:].rearrange("p t j -> p j t"))
             cols = slice(half * HALF, (half + 1) * HALF)
             nc.vector.quantize_mx(
                 out=h_codes[:, cols].bitcast(FP8X4), scales=h_scales[:, cols], in_=grouped[:].rearrange("p j t -> p (j t)")
             )
 
-        def up_tile(n, on_vector):
-            return interleave(on_vector, up_raw[n // 2][:, :, (n % 2) * P : (n % 2 + 1) * P], "up_bf%d" % n)
+        def quantize_up(n):
+            up_q[n] = quantize(interleave(n in UP_ON_V, up_raw[n], "up_bf%d" % n), "up%d" % n)
 
-        up_q = {}
-        quantize_h(0)
-        up_q[0] = quantize(up_tile(0, True), "up0")
-        up_q[1] = quantize(up_tile(1, True), "up1")
-        quantize_h(1)
-
-        def product(n, halves):
-            c = max(i for i, (lo, hi) in enumerate(w4_ranges) if lo <= n)
-            col = n - w4_ranges[c][0]
-            d = max(i for i, (lo, hi) in enumerate(scale_ranges) if lo <= n)
-            scol = n - scale_ranges[d][0]
-            width = HALF * len(halves)
-            cols = slice(halves[0] * HALF, halves[0] * HALF + width)
+        def product(n, lo, hi):
+            width = HALF * (hi - lo)
+            cols = slice(lo * HALF, hi * HALF)
             acc = y_psum.tile([P, width], F32, name="y_acc")
             for a in range(PASSES):
-                for i, half in enumerate(halves):
+                for half in range(lo, hi):
                     x_codes, x_scales = x_q[a, half]
                     nc.tensor.matmul_mx(
-                        out=acc[:, i * HALF : (i + 1) * HALF],
-                        lhsT=w4_code[c][:, a, 2 * P * col : 2 * P * (col + 1)].bitcast(FP4X4),
-                        lhsT_scale=w4_scale[d][:, a, P * scol : P * (scol + 1)],
+                        out=acc[:, (half - lo) * HALF : (half - lo + 1) * HALF],
+                        lhsT=w4_code[n][:, a, :].bitcast(FP4X4),
+                        lhsT_scale=w4_scale[n][:, a, :],
                         rhs=x_codes[:].bitcast(FP8X4),
                         rhs_scale=x_scales[:],
-                        start=(a == 0 and i == 0),
+                        start=(a == 0 and half == lo),
                         stop=False,
                     )
             nc.tensor.matmul_mx(
@@ -189,25 +205,21 @@ def tile_list_hscat_l_none_kernel(tc, x, w4_words, w4_scales, down, up, wgo, off
                 start=False,
                 stop=True,
             )
-            y = keep.tile([P, width], F32, name="y%d_%d" % (n, halves[0]))
-            nc.scalar.copy(out=y[:], in_=acc[:])
+            name = "y%d_%d" % (n, lo)
+            if TIES.get(name, "").startswith("up_bf"):
+                y = keep.tile([P, width], F32, name=name, tag=TIES[name], align_bytes=64)
+            else:
+                y = keep.tile([P, width], F32, name=name, tag=TIES.get(name, name))
+            cast((n, lo) in Y_ON_V, y[:], acc[:])
             nc.vector.tensor_tensor(
                 windows[n][:].indirect(offsets[:, cols.start // 16 : cols.stop // 16]),
                 y[:],
                 weights[:, cols],
                 mybir.AluOpType.mult,
             )
+            if hi == HALVES:
+                nc.sync.dma_start(out=out[n * P : (n + 1) * P, :], in_=windows[n][:])
 
-        def store(n):
-            nc.sync.dma_start(out=out[n * P : (n + 1) * P, :], in_=windows[n][:])
-
-        for half in range(HALVES):
-            for n in (0, 1):
-                product(n, [half])
-                if half == HALVES - 1:
-                    store(n)
-        for n in range(2, ROW_TILES):
-            up_q[n] = quantize(up_tile(n, False), "up%d" % n)
-        for n in range(2, ROW_TILES):
-            product(n, [0, 1])
-            store(n)
+        steps = {"qd": quantize_down, "qx": quantize_x, "h": h_pass, "warm": warm, "qh": quantize_h, "qu": quantize_up, "y": product}
+        for step in STEPS:
+            steps[step[0]](*step[1:])

@@ -21,15 +21,11 @@ PASSES = K // K_PASS
 HALF = 128
 HALVES = S // HALF
 ROW_TILES = M // P
-
-LOADS = [('down', 0), ('offs',), ('down', 1), ('down', 2), ('x', 0, 0, 2), ('x', 1, 0, 2), ('x', 2, 0, 2), ('up', 0, 2), ('w', 0, 2), ('sc', 0, 4), ('up', 2, 3), ('wgo',), ('up', 3, 4), ('w', 2, 4), ('up', 4, 6), ('sc', 4, 8), ('w', 4, 8), ('up', 6, 8)]
-POOL_MEMSETS = []
-X_ON_V = [(0, 0), (1, 0), (2, 0)]
-H_ON_V = []
-UP_ON_V = [0, 1, 2]
-Y_ON_V = []
-TIES = {}
-STEPS = [('qd', 0), ('qd', 1), ('qd', 2), ('qx', 0, 0), ('h', 0, 0), ('qx', 1, 0), ('h', 1, 0), ('qx', 2, 0), ('h', 2, 0), ('qh', 0), ('qu', 0), ('y', 0, 0, 1), ('qx', 0, 1), ('h', 0, 1), ('qx', 1, 1), ('h', 1, 1), ('qx', 2, 1), ('h', 2, 1), ('qu', 1), ('qh', 1), ('y', 1, 0, 1), ('y', 0, 1, 2), ('qu', 2), ('y', 1, 1, 2), ('qu', 3), ('y', 2, 0, 2), ('qu', 4), ('y', 3, 0, 2), ('qu', 5), ('y', 4, 0, 2), ('qu', 6), ('y', 5, 0, 2), ('qu', 7), ('y', 6, 0, 2), ('y', 7, 0, 2)]
+QUADRANTS = 4
+LINE = 4
+SCALE_TILES = 4
+VECTOR_UP_TILES = 3
+Y_BANKS = 6
 
 
 def tile_list_hscat_l_none_kernel(tc, x, w4_words, w4_scales, down, up, wgo, offs, out):
@@ -37,78 +33,83 @@ def tile_list_hscat_l_none_kernel(tc, x, w4_words, w4_scales, down, up, wgo, off
     with ExitStack() as ctx:
         keep = ctx.enter_context(tc.tile_pool(name="keep", bufs=1))
         h_psum = ctx.enter_context(tc.psum_pool(name="h_psum", bufs=1))
-        y_psum = ctx.enter_context(tc.psum_pool(name="y_psum", bufs=6))
+        y_psum = ctx.enter_context(tc.psum_pool(name="y_psum", bufs=Y_BANKS))
 
         offsets = keep.tile([P, S // 16], U16, name="offsets")
         weights = keep.tile([P, S], F32, name="weights")
         windows = [keep.tile([P, T], F32, name="window%d" % n) for n in range(ROW_TILES)]
+
         scale_tile = {}
-        for item in LOADS:
-            if item[0] == "sc":
-                lo, hi = item[1:]
-                plane = keep.tile([P, PASSES, P * (hi - lo)], U8, name="w4_scale%d" % lo, align_bytes=64)
-                nc.vector.memset(plane[:].rearrange("p a n -> p (a n)").bitcast(U32), 0)
-                scale_tile[lo] = plane
-        for n, window in enumerate(windows):
-            (nc.gpsimd if n in POOL_MEMSETS else nc.vector).memset(window[:], 0.0)
+        for lo in range(0, ROW_TILES, SCALE_TILES):
+            scale_tile[lo] = keep.tile([P, PASSES, P * SCALE_TILES], U8, name="w4_scale%d" % lo, align_bytes=64)
+            nc.vector.memset(scale_tile[lo][:].rearrange("p a n -> p (a n)").bitcast(U32), 0)
+        for window in windows:
+            nc.vector.memset(window[:], 0.0)
+
+        down_raw, x_raw, up_raw, w4_code, w4_scale = {}, {}, {}, {}, {}
 
         def load_rows(rows, name):
-            raw = keep.tile([P, PACK, rows.shape[1]], F32, name=name, tag=name)
+            raw = keep.tile([P, PACK, rows.shape[1]], F32, name=name)
             nc.sync.dma_start(out=raw[:], in_=rows.rearrange("(p i) c -> p i c", i=PACK))
             return raw
 
-        down_raw, x_raw, up_raw, w4_code, w4_scale = {}, {}, {}, {}, {}
-        for item in LOADS:
-            kind = item[0]
-            if kind == "offs":
-                nc.sync.dma_start(offsets[:], offs)
-            elif kind == "wgo":
-                nc.sync.dma_start(out=weights[:], in_=wgo)
-            elif kind == "down":
-                a = item[1]
-                down_raw[a] = load_rows(down[a * K_PASS : (a + 1) * K_PASS, :], "down_raw%d" % a)
-            elif kind == "x":
-                a, lo, hi = item[1:]
-                raw = load_rows(x[a * K_PASS : (a + 1) * K_PASS, lo * HALF : hi * HALF], "x_raw%d_%d" % (a, lo))
-                for half in range(lo, hi):
-                    x_raw[a, half] = raw[:, :, (half - lo) * HALF : (half - lo + 1) * HALF]
-            elif kind == "up":
-                lo, hi = item[1:]
-                raw = load_rows(up[:, lo * P : hi * P], "up_raw%d" % lo)
-                for n in range(lo, hi):
-                    up_raw[n] = raw[:, :, (n - lo) * P : (n - lo + 1) * P]
-            elif kind == "sc":
-                lo, hi = item[1:]
-                for q in range(4):
-                    nc.sync.dma_start(
-                        out=scale_tile[lo][32 * q : 32 * q + 4, :, :].bitcast(I32),
-                        in_=w4_scales[:, 4 * q : 4 * q + 4, P * lo : P * hi].rearrange("a r n -> r a n").bitcast(I32),
-                    )
-                for n in range(lo, hi):
-                    w4_scale[n] = scale_tile[lo][:, :, (n - lo) * P : (n - lo + 1) * P]
-            else:
-                lo, hi = item[1:]
-                codes = keep.tile([P, PASSES, 2 * P * (hi - lo)], U8, name="w4_code%d" % lo, align_bytes=64)
+        def load_down(a):
+            down_raw[a] = load_rows(down[a * K_PASS : (a + 1) * K_PASS, :], "down_raw%d" % a)
+
+        def load_x(a):
+            raw = load_rows(x[a * K_PASS : (a + 1) * K_PASS, :], "x_raw%d_0" % a)
+            for half in range(HALVES):
+                x_raw[a, half] = raw[:, :, half * HALF : (half + 1) * HALF]
+
+        def load_up(lo, hi):
+            raw = load_rows(up[:, lo * P : hi * P], "up_raw%d" % lo)
+            for n in range(lo, hi):
+                up_raw[n] = raw[:, :, (n - lo) * P : (n - lo + 1) * P]
+
+        def load_codes(lo, hi):
+            codes = keep.tile([P, PASSES, 2 * P * (hi - lo)], U8, name="w4_code%d" % lo, align_bytes=64)
+            nc.sync.dma_start(
+                out=codes[:].bitcast(I32),
+                in_=w4_words[:, :, 2 * P * lo : 2 * P * hi].rearrange("a p n -> p a n").bitcast(I32),
+            )
+            for n in range(lo, hi):
+                w4_code[n] = codes[:, :, (n - lo) * 2 * P : (n - lo + 1) * 2 * P]
+
+        def load_scales(lo):
+            hi = lo + SCALE_TILES
+            for q in range(QUADRANTS):
                 nc.sync.dma_start(
-                    out=codes[:].bitcast(I32),
-                    in_=w4_words[:, :, 2 * P * lo : 2 * P * hi].rearrange("a p n -> p a n").bitcast(I32),
+                    out=scale_tile[lo][32 * q : 32 * q + 4, :, :].bitcast(I32),
+                    in_=w4_scales[:, 4 * q : 4 * q + 4, P * lo : P * hi].rearrange("a r n -> r a n").bitcast(I32),
                 )
-                for n in range(lo, hi):
-                    w4_code[n] = codes[:, :, (n - lo) * 2 * P : (n - lo + 1) * 2 * P]
+            for n in range(lo, hi):
+                w4_scale[n] = scale_tile[lo][:, :, (n - lo) * P : (n - lo + 1) * P]
 
-        def cast(on_vector, dst, src):
-            if on_vector:
-                nc.vector.tensor_copy(out=dst, in_=src)
-            else:
-                nc.scalar.copy(out=dst, in_=src)
+        load_down(0)
+        nc.sync.dma_start(offsets[:], offs)
+        for a in range(1, PASSES):
+            load_down(a)
+        for a in range(PASSES):
+            load_x(a)
+        load_up(0, 2)
+        load_codes(0, 2)
+        load_scales(0)
+        load_up(2, 3)
+        nc.sync.dma_start(out=weights[:], in_=wgo)
+        load_up(3, 4)
+        load_codes(2, 4)
+        load_up(4, 6)
+        load_scales(SCALE_TILES)
+        load_codes(4, 8)
+        load_up(6, 8)
 
-        def interleave(on_vector, raw_cols, name):
-            width = raw_cols.shape[2]
-            grouped = keep.tile([P, width, PACK], BF16, name=name, tag=name, align_bytes=64)
-            cast(
-                on_vector,
-                grouped[:].rearrange("p (c e) i -> p c i e", e=4),
-                raw_cols.rearrange("p i (c e) -> p c i e", e=4),
+        on_vector, on_scalar = nc.vector.tensor_copy, nc.scalar.copy
+
+        def interleave(copy, raw_cols, name, run=LINE):
+            grouped = keep.tile([P, raw_cols.shape[2], PACK], BF16, name=name, align_bytes=64)
+            copy(
+                out=grouped[:].rearrange("p (c e) i -> p c i e", e=run),
+                in_=raw_cols.rearrange("p i (c e) -> p c i e", e=run),
             )
             return grouped[:].rearrange("p c i -> p (c i)")
 
@@ -126,59 +127,45 @@ def tile_list_hscat_l_none_kernel(tc, x, w4_words, w4_scales, down, up, wgo, off
 
         def quantize_down(a):
             flats = {}
-            for tp in (1, 0):
-                grouped = keep.tile([P, 2, P, PACK], BF16, name="down_bf%d_%d" % (a, tp), align_bytes=64)
-                cast(
-                    tp == 1,
-                    grouped[:].rearrange("p t m i -> p m i t"),
-                    down_raw[a][:].rearrange("p i (m t) -> p m i t", t=PACK)[:, :, :, 2 * tp : 2 * tp + 2],
+            for pair, copy in ((1, on_vector), (0, on_scalar)):
+                grouped = keep.tile([P, 2, P, PACK], BF16, name="down_bf%d_%d" % (a, pair), align_bytes=64)
+                copy(
+                    out=grouped[:].rearrange("p t m i -> p m i t"),
+                    in_=down_raw[a][:].rearrange("p i (m t) -> p m i t", t=PACK)[:, :, :, 2 * pair : 2 * pair + 2],
                 )
-                flats[tp] = grouped[:].rearrange("p t m i -> p (t m i)")
-            for tp in (1, 0):
-                down_q[a, tp] = quantize(flats[tp], "down%d_%d" % (a, tp))
+                flats[pair] = grouped[:].rearrange("p t m i -> p (t m i)")
+            for pair in (1, 0):
+                down_q[a, pair] = quantize(flats[pair], "down%d_%d" % (a, pair))
 
-        def quantize_x(a, half):
-            x_q[a, half] = quantize(interleave((a, half) in X_ON_V, x_raw[a, half], "x_bf%d_%d" % (a, half)), "x%d_%d" % (a, half))
-
-        def h_pass(a, half):
-            x_codes, x_scales = x_q[a, half]
-            for t in range(PACK):
-                d_codes, d_scales = down_q[a, t // 2]
-                cols = slice((t % 2) * P, (t % 2 + 1) * P)
-                nc.tensor.matmul_mx(
-                    out=h_acc[half][:, t, :],
-                    lhsT=d_codes[:, cols].bitcast(FP8X4),
-                    lhsT_scale=d_scales[:, cols],
-                    rhs=x_codes[:].bitcast(FP8X4),
-                    rhs_scale=x_scales[:],
-                    start=(a == 0 and t == 0),
-                    stop=(a == PASSES - 1 and t == PACK - 1),
+        def half_of_h(half, copy):
+            for a in range(PASSES):
+                x_codes, x_scales = x_q[a, half] = quantize(
+                    interleave(copy, x_raw[a, half], "x_bf%d_%d" % (a, half)), "x%d_%d" % (a, half)
                 )
-
-        def warm(a, tp, count):
-            codes, scales = down_q[a, tp]
-            for i in range(count):
-                acc = y_psum.tile([P, 2 * P], F32, name="y_acc")
-                nc.tensor.matmul_mx(
-                    out=acc[:],
-                    lhsT=codes[:, 0:P].bitcast(FP8X4),
-                    lhsT_scale=scales[:, 0:P],
-                    rhs=codes[:].bitcast(FP8X4),
-                    rhs_scale=scales[:],
-                    start=True,
-                    stop=True,
-                )
+                for t in range(PACK):
+                    d_codes, d_scales = down_q[a, t // 2]
+                    cols = slice((t % 2) * P, (t % 2 + 1) * P)
+                    nc.tensor.matmul_mx(
+                        out=h_acc[half][:, t, :],
+                        lhsT=d_codes[:, cols].bitcast(FP8X4),
+                        lhsT_scale=d_scales[:, cols],
+                        rhs=x_codes[:].bitcast(FP8X4),
+                        rhs_scale=x_scales[:],
+                        start=(a == 0 and t == 0),
+                        stop=(a == PASSES - 1 and t == PACK - 1),
+                    )
 
         def quantize_h(half):
             grouped = keep.tile([P, HALF, PACK], BF16, name="h_bf%d" % half, align_bytes=64)
-            cast(half in H_ON_V, grouped[:], h_acc[half][:].rearrange("p t j -> p j t"))
+            on_scalar(out=grouped[:], in_=h_acc[half][:].rearrange("p t j -> p j t"))
             cols = slice(half * HALF, (half + 1) * HALF)
             nc.vector.quantize_mx(
                 out=h_codes[:, cols].bitcast(FP8X4), scales=h_scales[:, cols], in_=grouped[:].rearrange("p j t -> p (j t)")
             )
 
         def quantize_up(n):
-            up_q[n] = quantize(interleave(n in UP_ON_V, up_raw[n], "up_bf%d" % n), "up%d" % n)
+            copy, run = (on_vector, LINE) if n < VECTOR_UP_TILES else (on_scalar, 1)
+            up_q[n] = quantize(interleave(copy, up_raw[n], "up_bf%d" % n, run), "up%d" % n)
 
         def product(n, lo, hi):
             width = HALF * (hi - lo)
@@ -205,12 +192,8 @@ def tile_list_hscat_l_none_kernel(tc, x, w4_words, w4_scales, down, up, wgo, off
                 start=False,
                 stop=True,
             )
-            name = "y%d_%d" % (n, lo)
-            if TIES.get(name, "").startswith("up_bf"):
-                y = keep.tile([P, width], F32, name=name, tag=TIES[name], align_bytes=64)
-            else:
-                y = keep.tile([P, width], F32, name=name, tag=TIES.get(name, name))
-            cast((n, lo) in Y_ON_V, y[:], acc[:])
+            y = keep.tile([P, width], F32, name="y%d_%d" % (n, lo))
+            on_scalar(out=y[:], in_=acc[:])
             nc.vector.tensor_tensor(
                 windows[n][:].indirect(offsets[:, cols.start // 16 : cols.stop // 16]),
                 y[:],
@@ -220,6 +203,20 @@ def tile_list_hscat_l_none_kernel(tc, x, w4_words, w4_scales, down, up, wgo, off
             if hi == HALVES:
                 nc.sync.dma_start(out=out[n * P : (n + 1) * P, :], in_=windows[n][:])
 
-        steps = {"qd": quantize_down, "qx": quantize_x, "h": h_pass, "warm": warm, "qh": quantize_h, "qu": quantize_up, "y": product}
-        for step in STEPS:
-            steps[step[0]](*step[1:])
+        for a in range(PASSES):
+            quantize_down(a)
+        half_of_h(0, on_vector)
+        quantize_h(0)
+        quantize_up(0)
+        product(0, 0, 1)
+        half_of_h(1, on_scalar)
+        quantize_up(1)
+        quantize_h(1)
+        product(1, 0, 1)
+        product(0, 1, 2)
+        quantize_up(2)
+        product(1, 1, 2)
+        for n in range(2, ROW_TILES):
+            if n + 1 < ROW_TILES:
+                quantize_up(n + 1)
+            product(n, 0, HALVES)

@@ -23,7 +23,7 @@ HALVES = S // HALF
 ROW_TILES = M // P
 QUADRANTS = 4
 LINE = 4
-SCALE_TILES = 4
+EARLY_TILES = 2
 VECTOR_UP_TILES = 3
 Y_BANKS = 6
 
@@ -40,8 +40,8 @@ def tile_list_hscat_l_none_kernel(tc, x, w4_words, w4_scales, down, up, wgo, off
         windows = [keep.tile([P, T], F32, name="window%d" % n) for n in range(ROW_TILES)]
 
         scale_tile = {}
-        for lo in range(0, ROW_TILES, SCALE_TILES):
-            scale_tile[lo] = keep.tile([P, PASSES, P * SCALE_TILES], U8, name="w4_scale%d" % lo, align_bytes=64)
+        for lo, hi in ((0, EARLY_TILES), (EARLY_TILES, ROW_TILES)):
+            scale_tile[lo] = keep.tile([P, PASSES, P * (hi - lo)], U8, name="w4_scale%d" % lo, align_bytes=64)
             nc.vector.memset(scale_tile[lo][:].rearrange("p a n -> p (a n)").bitcast(U32), 0)
         for window in windows:
             nc.vector.memset(window[:], 0.0)
@@ -53,8 +53,12 @@ def tile_list_hscat_l_none_kernel(tc, x, w4_words, w4_scales, down, up, wgo, off
             nc.sync.dma_start(out=raw[:], in_=rows.rearrange("(p i) c -> p i c", i=PACK))
             return raw
 
-        def load_down(a):
-            down_raw[a] = load_rows(down[a * K_PASS : (a + 1) * K_PASS, :], "down_raw%d" % a)
+        def load_down(lo, hi):
+            raw = keep.tile([P, hi - lo, PACK * R], F32, name="down_raw%d" % lo)
+            rows = down[lo * K_PASS : hi * K_PASS, :]
+            nc.sync.dma_start(out=raw[:], in_=rows.rearrange("(a p i) c -> p a (i c)", p=P, i=PACK))
+            for a in range(lo, hi):
+                down_raw[a] = raw[:, a - lo, :]
 
         def load_x(a):
             raw = load_rows(x[a * K_PASS : (a + 1) * K_PASS, :], "x_raw%d_0" % a)
@@ -75,31 +79,29 @@ def tile_list_hscat_l_none_kernel(tc, x, w4_words, w4_scales, down, up, wgo, off
             for n in range(lo, hi):
                 w4_code[n] = codes[:, :, (n - lo) * 2 * P : (n - lo + 1) * 2 * P]
 
-        def load_scales(lo):
-            hi = lo + SCALE_TILES
-            for q in range(QUADRANTS):
+        def load_scales(lo, hi):
+            for r in range(4):
                 nc.sync.dma_start(
-                    out=scale_tile[lo][32 * q : 32 * q + 4, :, :].bitcast(I32),
-                    in_=w4_scales[:, 4 * q : 4 * q + 4, P * lo : P * hi].rearrange("a r n -> r a n").bitcast(I32),
+                    out=scale_tile[lo][r:P:32, :, :].bitcast(I32),
+                    in_=w4_scales[:, r:16:4, P * lo : P * hi].rearrange("a q n -> q a n").bitcast(I32),
                 )
             for n in range(lo, hi):
                 w4_scale[n] = scale_tile[lo][:, :, (n - lo) * P : (n - lo + 1) * P]
 
-        load_down(0)
-        nc.sync.dma_start(offsets[:], offs)
-        for a in range(1, PASSES):
-            load_down(a)
+        for a in range(PASSES):
+            load_down(a, a + 1)
         for a in range(PASSES):
             load_x(a)
         load_up(0, 2)
-        load_codes(0, 2)
-        load_scales(0)
         load_up(2, 3)
+        load_codes(0, 2)
+        load_scales(0, EARLY_TILES)
         nc.sync.dma_start(out=weights[:], in_=wgo)
+        nc.sync.dma_start(offsets[:], offs)
         load_up(3, 4)
         load_codes(2, 4)
+        load_scales(EARLY_TILES, ROW_TILES)
         load_up(4, 6)
-        load_scales(SCALE_TILES)
         load_codes(4, 8)
         load_up(6, 8)
 
@@ -131,7 +133,7 @@ def tile_list_hscat_l_none_kernel(tc, x, w4_words, w4_scales, down, up, wgo, off
                 grouped = keep.tile([P, 2, P, PACK], BF16, name="down_bf%d_%d" % (a, pair), align_bytes=64)
                 copy(
                     out=grouped[:].rearrange("p t m i -> p m i t"),
-                    in_=down_raw[a][:].rearrange("p i (m t) -> p m i t", t=PACK)[:, :, :, 2 * pair : 2 * pair + 2],
+                    in_=down_raw[a].rearrange("p (i m t) -> p m i t", i=PACK, t=PACK)[:, :, :, 2 * pair : 2 * pair + 2],
                 )
                 flats[pair] = grouped[:].rearrange("p t m i -> p (t m i)")
             for pair in (1, 0):

@@ -23,7 +23,7 @@ HALVES = S // HALF
 ROW_TILES = M // P
 QUADRANTS = 4
 LINE = 4
-EARLY_TILES = 2
+FIRST_SCALE_TILES = 3
 VECTOR_UP_TILES = 3
 Y_BANKS = 6
 
@@ -40,7 +40,7 @@ def tile_list_hscat_l_none_kernel(tc, x, w4_words, w4_scales, down, up, wgo, off
         windows = [keep.tile([P, T], F32, name="window%d" % n) for n in range(ROW_TILES)]
 
         scale_tile = {}
-        for lo, hi in ((0, EARLY_TILES), (EARLY_TILES, ROW_TILES)):
+        for lo, hi in ((0, FIRST_SCALE_TILES), (FIRST_SCALE_TILES, ROW_TILES)):
             scale_tile[lo] = keep.tile([P, PASSES, P * (hi - lo)], U8, name="w4_scale%d" % lo, align_bytes=64)
             nc.vector.memset(scale_tile[lo][:].rearrange("p a n -> p (a n)").bitcast(U32), 0)
         for window in windows:
@@ -48,9 +48,9 @@ def tile_list_hscat_l_none_kernel(tc, x, w4_words, w4_scales, down, up, wgo, off
 
         down_raw, x_raw, up_raw, w4_code, w4_scale = {}, {}, {}, {}, {}
 
-        def load_rows(rows, name):
-            raw = keep.tile([P, PACK, rows.shape[1]], F32, name=name)
-            nc.sync.dma_start(out=raw[:], in_=rows.rearrange("(p i) c -> p i c", i=PACK))
+        def load_rows(rows, name, queue=nc.sync):
+            raw = keep.tile([P, PACK, rows.shape[1]], F32, name=name, align_bytes=64)
+            queue.dma_start(out=raw[:], in_=rows.rearrange("(p i) c -> p i c", i=PACK))
             return raw
 
         def load_down(lo, hi):
@@ -93,15 +93,14 @@ def tile_list_hscat_l_none_kernel(tc, x, w4_words, w4_scales, down, up, wgo, off
         for a in range(PASSES):
             load_x(a)
         load_up(0, 2)
-        load_up(2, 3)
         load_codes(0, 2)
-        load_scales(0, EARLY_TILES)
+        load_scales(0, FIRST_SCALE_TILES)
         nc.sync.dma_start(out=weights[:], in_=wgo)
         nc.sync.dma_start(offsets[:], offs)
         load_up(3, 4)
         load_codes(2, 4)
-        load_scales(EARLY_TILES, ROW_TILES)
         load_up(4, 6)
+        load_scales(FIRST_SCALE_TILES, ROW_TILES)
         load_codes(4, 8)
         load_up(6, 8)
 
@@ -212,6 +211,7 @@ def tile_list_hscat_l_none_kernel(tc, x, w4_words, w4_scales, down, up, wgo, off
         quantize_up(0)
         product(0, 0, 1)
         half_of_h(1, on_scalar)
+        up_raw[2] = load_rows(up[:, 2 * P : 3 * P], "x_bf1_0", nc.scalar)[:]
         quantize_up(1)
         quantize_h(1)
         product(1, 0, 1)

@@ -23,8 +23,9 @@ HALVES = S // HALF
 ROW_TILES = M // P
 QUADRANTS = 4
 LINE = 4
-FIRST_SCALE_TILES = 3
+FIRST_SCALE_TILES = 2
 VECTOR_UP_TILES = 3
+WARM_UPS = 2
 Y_BANKS = 6
 
 
@@ -88,19 +89,20 @@ def tile_list_hscat_l_none_kernel(tc, x, w4_words, w4_scales, down, up, wgo, off
             for n in range(lo, hi):
                 w4_scale[n] = scale_tile[lo][:, :, (n - lo) * P : (n - lo + 1) * P]
 
-        for a in range(PASSES):
+        load_down(0, 1)
+        nc.sync.dma_start(offsets[:], offs)
+        for a in range(1, PASSES):
             load_down(a, a + 1)
         for a in range(PASSES):
             load_x(a)
         load_up(0, 2)
-        load_codes(0, 2)
         load_scales(0, FIRST_SCALE_TILES)
+        load_codes(0, 2)
         nc.sync.dma_start(out=weights[:], in_=wgo)
-        nc.sync.dma_start(offsets[:], offs)
         load_up(3, 4)
+        load_scales(FIRST_SCALE_TILES, ROW_TILES)
         load_codes(2, 4)
         load_up(4, 6)
-        load_scales(FIRST_SCALE_TILES, ROW_TILES)
         load_codes(4, 8)
         load_up(6, 8)
 
@@ -206,6 +208,18 @@ def tile_list_hscat_l_none_kernel(tc, x, w4_words, w4_scales, down, up, wgo, off
 
         for a in range(PASSES):
             quantize_down(a)
+        codes, scales = down_q[PASSES - 1, 1]
+        unread = y_psum.tile([P, 2 * P], F32, name="y_acc")
+        for warm_up in range(WARM_UPS):
+            nc.tensor.matmul_mx(
+                out=unread[:],
+                lhsT=codes[:, 0:P].bitcast(FP8X4),
+                lhsT_scale=scales[:, 0:P],
+                rhs=codes[:].bitcast(FP8X4),
+                rhs_scale=scales[:],
+                start=True,
+                stop=True,
+            )
         half_of_h(0, on_vector)
         quantize_h(0)
         quantize_up(0)

@@ -21,9 +21,11 @@ PASSES = K // K_PASS
 HALF = 128
 HALVES = S // HALF
 ROW_TILES = M // P
-QUADRANTS = 4
+GROUP = 16
+QUADRANT = 32
+SCALE_ROWS = 4
 LINE = 4
-FIRST_SCALE_TILES = 2
+EARLY_TILES = 2
 VECTOR_UP_TILES = 3
 WARM_UPS = 2
 Y_BANKS = 6
@@ -36,12 +38,12 @@ def tile_list_hscat_l_none_kernel(tc, x, w4_words, w4_scales, down, up, wgo, off
         h_psum = ctx.enter_context(tc.psum_pool(name="h_psum", bufs=1))
         y_psum = ctx.enter_context(tc.psum_pool(name="y_psum", bufs=Y_BANKS))
 
-        offsets = keep.tile([P, S // 16], U16, name="offsets")
+        offsets = keep.tile([P, S // GROUP], U16, name="offsets")
         weights = keep.tile([P, S], F32, name="weights")
         windows = [keep.tile([P, T], F32, name="window%d" % n) for n in range(ROW_TILES)]
 
         scale_tile = {}
-        for lo, hi in ((0, FIRST_SCALE_TILES), (FIRST_SCALE_TILES, ROW_TILES)):
+        for lo, hi in ((0, EARLY_TILES), (EARLY_TILES, ROW_TILES)):
             scale_tile[lo] = keep.tile([P, PASSES, P * (hi - lo)], U8, name="w4_scale%d" % lo, align_bytes=64)
             nc.vector.memset(scale_tile[lo][:].rearrange("p a n -> p (a n)").bitcast(U32), 0)
         for window in windows:
@@ -49,25 +51,13 @@ def tile_list_hscat_l_none_kernel(tc, x, w4_words, w4_scales, down, up, wgo, off
 
         down_raw, x_raw, up_raw, w4_code, w4_scale = {}, {}, {}, {}, {}
 
-        def load_rows(rows, name, queue=nc.sync):
+        def load_rows(rows, name, queue):
             raw = keep.tile([P, PACK, rows.shape[1]], F32, name=name, align_bytes=64)
             queue.dma_start(out=raw[:], in_=rows.rearrange("(p i) c -> p i c", i=PACK))
             return raw
 
-        def load_down(lo, hi):
-            raw = keep.tile([P, hi - lo, PACK * R], F32, name="down_raw%d" % lo)
-            rows = down[lo * K_PASS : hi * K_PASS, :]
-            nc.sync.dma_start(out=raw[:], in_=rows.rearrange("(a p i) c -> p a (i c)", p=P, i=PACK))
-            for a in range(lo, hi):
-                down_raw[a] = raw[:, a - lo, :]
-
-        def load_x(a):
-            raw = load_rows(x[a * K_PASS : (a + 1) * K_PASS, :], "x_raw%d_0" % a)
-            for half in range(HALVES):
-                x_raw[a, half] = raw[:, :, half * HALF : (half + 1) * HALF]
-
         def load_up(lo, hi):
-            raw = load_rows(up[:, lo * P : hi * P], "up_raw%d" % lo)
+            raw = load_rows(up[:, lo * P : hi * P], "up_raw%d" % lo, nc.sync)
             for n in range(lo, hi):
                 up_raw[n] = raw[:, :, (n - lo) * P : (n - lo + 1) * P]
 
@@ -81,26 +71,28 @@ def tile_list_hscat_l_none_kernel(tc, x, w4_words, w4_scales, down, up, wgo, off
                 w4_code[n] = codes[:, :, (n - lo) * 2 * P : (n - lo + 1) * 2 * P]
 
         def load_scales(lo, hi):
-            for r in range(4):
+            for row in range(SCALE_ROWS):
+                rows = w4_scales[:, row::SCALE_ROWS, P * lo : P * hi]
                 nc.sync.dma_start(
-                    out=scale_tile[lo][r:P:32, :, :].bitcast(I32),
-                    in_=w4_scales[:, r:16:4, P * lo : P * hi].rearrange("a q n -> q a n").bitcast(I32),
+                    out=scale_tile[lo][row:P:QUADRANT, :, :].bitcast(I32),
+                    in_=rows.rearrange("a q n -> q a n").bitcast(I32),
                 )
             for n in range(lo, hi):
                 w4_scale[n] = scale_tile[lo][:, :, (n - lo) * P : (n - lo + 1) * P]
 
-        load_down(0, 1)
-        nc.sync.dma_start(offsets[:], offs)
-        for a in range(1, PASSES):
-            load_down(a, a + 1)
         for a in range(PASSES):
-            load_x(a)
-        load_up(0, 2)
-        load_scales(0, FIRST_SCALE_TILES)
-        load_codes(0, 2)
+            down_raw[a] = load_rows(down[a * K_PASS : (a + 1) * K_PASS, :], "down_raw%d" % a, nc.sync)
+        for a in range(PASSES):
+            raw = load_rows(x[a * K_PASS : (a + 1) * K_PASS, :], "x_raw%d" % a, nc.sync)
+            for half in range(HALVES):
+                x_raw[a, half] = raw[:, :, half * HALF : (half + 1) * HALF]
+        load_up(0, EARLY_TILES)
+        load_scales(0, EARLY_TILES)
+        load_codes(0, EARLY_TILES)
         nc.sync.dma_start(out=weights[:], in_=wgo)
+        nc.sync.dma_start(offsets[:], offs)
         load_up(3, 4)
-        load_scales(FIRST_SCALE_TILES, ROW_TILES)
+        load_scales(EARLY_TILES, ROW_TILES)
         load_codes(2, 4)
         load_up(4, 6)
         load_codes(4, 8)
@@ -134,7 +126,7 @@ def tile_list_hscat_l_none_kernel(tc, x, w4_words, w4_scales, down, up, wgo, off
                 grouped = keep.tile([P, 2, P, PACK], BF16, name="down_bf%d_%d" % (a, pair), align_bytes=64)
                 copy(
                     out=grouped[:].rearrange("p t m i -> p m i t"),
-                    in_=down_raw[a].rearrange("p (i m t) -> p m i t", i=PACK, t=PACK)[:, :, :, 2 * pair : 2 * pair + 2],
+                    in_=down_raw[a][:].rearrange("p i (m t) -> p m i t", t=PACK)[:, :, :, 2 * pair : 2 * pair + 2],
                 )
                 flats[pair] = grouped[:].rearrange("p t m i -> p (t m i)")
             for pair in (1, 0):
@@ -198,7 +190,7 @@ def tile_list_hscat_l_none_kernel(tc, x, w4_words, w4_scales, down, up, wgo, off
             y = keep.tile([P, width], F32, name="y%d_%d" % (n, lo))
             on_scalar(out=y[:], in_=acc[:])
             nc.vector.tensor_tensor(
-                windows[n][:].indirect(offsets[:, cols.start // 16 : cols.stop // 16]),
+                windows[n][:].indirect(offsets[:, cols.start // GROUP : cols.stop // GROUP]),
                 y[:],
                 weights[:, cols],
                 mybir.AluOpType.mult,
@@ -208,15 +200,15 @@ def tile_list_hscat_l_none_kernel(tc, x, w4_words, w4_scales, down, up, wgo, off
 
         for a in range(PASSES):
             quantize_down(a)
-        codes, scales = down_q[PASSES - 1, 1]
+        warm_codes, warm_scales = down_q[PASSES - 1, 1]
         unread = y_psum.tile([P, 2 * P], F32, name="y_acc")
         for warm_up in range(WARM_UPS):
             nc.tensor.matmul_mx(
                 out=unread[:],
-                lhsT=codes[:, 0:P].bitcast(FP8X4),
-                lhsT_scale=scales[:, 0:P],
-                rhs=codes[:].bitcast(FP8X4),
-                rhs_scale=scales[:],
+                lhsT=warm_codes[:, 0:P].bitcast(FP8X4),
+                lhsT_scale=warm_scales[:, 0:P],
+                rhs=warm_codes[:].bitcast(FP8X4),
+                rhs_scale=warm_scales[:],
                 start=True,
                 stop=True,
             )
@@ -232,7 +224,7 @@ def tile_list_hscat_l_none_kernel(tc, x, w4_words, w4_scales, down, up, wgo, off
         product(0, 1, 2)
         quantize_up(2)
         product(1, 1, 2)
-        for n in range(2, ROW_TILES):
+        for n in range(EARLY_TILES, ROW_TILES):
             if n + 1 < ROW_TILES:
                 quantize_up(n + 1)
             product(n, 0, HALVES)

@@ -27,7 +27,6 @@ SCALE_ROWS = 4
 LINE = 4
 EARLY_TILES = 2
 VECTOR_UP_TILES = 3
-WARM_UPS = 2
 Y_BANKS = 6
 
 
@@ -200,18 +199,6 @@ def tile_list_hscat_l_none_kernel(tc, x, w4_words, w4_scales, down, up, wgo, off
 
         for a in range(PASSES):
             quantize_down(a)
-        warm_codes, warm_scales = down_q[PASSES - 1, 1]
-        unread = y_psum.tile([P, 2 * P], F32, name="y_acc")
-        for warm_up in range(WARM_UPS):
-            nc.tensor.matmul_mx(
-                out=unread[:],
-                lhsT=warm_codes[:, 0:P].bitcast(FP8X4),
-                lhsT_scale=warm_scales[:, 0:P],
-                rhs=warm_codes[:].bitcast(FP8X4),
-                rhs_scale=warm_scales[:],
-                start=True,
-                stop=True,
-            )
         half_of_h(0, on_vector)
         quantize_h(0)
         quantize_up(0)

@@ -25,8 +25,8 @@ GROUP = 16
 QUADRANT = 32
 SCALE_ROWS = 4
 LINE = 4
-EARLY_TILES = 2
-VECTOR_UP_TILES = 3
+PAIR = 2
+EARLY_SCALES = 3
 Y_BANKS = 6
 
 
@@ -42,23 +42,29 @@ def tile_list_hscat_l_none_kernel(tc, x, w4_words, w4_scales, down, up, wgo, off
         windows = [keep.tile([P, T], F32, name="window%d" % n) for n in range(ROW_TILES)]
 
         scale_tile = {}
-        for lo, hi in ((0, EARLY_TILES), (EARLY_TILES, ROW_TILES)):
+        for lo, hi in ((0, EARLY_SCALES), (EARLY_SCALES, ROW_TILES)):
             scale_tile[lo] = keep.tile([P, PASSES, P * (hi - lo)], U8, name="w4_scale%d" % lo, align_bytes=64)
             nc.vector.memset(scale_tile[lo][:].rearrange("p a n -> p (a n)").bitcast(U32), 0)
         for window in windows:
             nc.vector.memset(window[:], 0.0)
 
-        down_raw, x_raw, up_raw, w4_code, w4_scale = {}, {}, {}, {}, {}
+        down_raw, x_raw, up_raw, up_bytes, w4_code, w4_scale = {}, {}, {}, {}, {}, {}
 
-        def load_rows(rows, name, queue):
-            raw = keep.tile([P, PACK, rows.shape[1]], F32, name=name, align_bytes=64)
-            queue.dma_start(out=raw[:], in_=rows.rearrange("(p i) c -> p i c", i=PACK))
+        def load_rows(rows, raw):
+            nc.sync.dma_start(out=raw, in_=rows.rearrange("(p i) c -> p i c", i=PACK))
+
+        def load_pass(source, a, name):
+            raw = keep.tile([P, PACK, source.shape[1]], F32, name="%s%d" % (name, a), align_bytes=64)
+            load_rows(source[a * K_PASS : (a + 1) * K_PASS, :], raw[:])
             return raw
 
-        def load_up(lo, hi):
-            raw = load_rows(up[:, lo * P : hi * P], "up_raw%d" % lo, nc.sync)
-            for n in range(lo, hi):
-                up_raw[n] = raw[:, :, (n - lo) * P : (n - lo + 1) * P]
+        def load_up(lo):
+            loaded = PACK * PAIR * P
+            room = keep.tile([P, HALF + loaded + HALF], F32, name="up_room%d" % lo, align_bytes=64)
+            raw = room[:, HALF : HALF + loaded].rearrange("p (i c) -> p i c", i=PACK)
+            load_rows(up[:, lo * P : (lo + PAIR) * P], raw)
+            up_raw[lo], up_raw[lo + 1] = raw[:, :, :P], raw[:, :, P:]
+            up_bytes[lo], up_bytes[lo + 1] = room[:, :S], room[:, loaded : loaded + S]
 
         def load_codes(lo, hi):
             codes = keep.tile([P, PASSES, 2 * P * (hi - lo)], U8, name="w4_code%d" % lo, align_bytes=64)
@@ -79,23 +85,23 @@ def tile_list_hscat_l_none_kernel(tc, x, w4_words, w4_scales, down, up, wgo, off
             for n in range(lo, hi):
                 w4_scale[n] = scale_tile[lo][:, :, (n - lo) * P : (n - lo + 1) * P]
 
-        for a in range(PASSES):
-            down_raw[a] = load_rows(down[a * K_PASS : (a + 1) * K_PASS, :], "down_raw%d" % a, nc.sync)
-        for a in range(PASSES):
-            raw = load_rows(x[a * K_PASS : (a + 1) * K_PASS, :], "x_raw%d" % a, nc.sync)
-            for half in range(HALVES):
-                x_raw[a, half] = raw[:, :, half * HALF : (half + 1) * HALF]
-        load_up(0, EARLY_TILES)
-        load_scales(0, EARLY_TILES)
-        load_codes(0, EARLY_TILES)
-        nc.sync.dma_start(out=weights[:], in_=wgo)
+        down_raw[0] = load_pass(down, 0, "down_raw")
+        load_scales(0, EARLY_SCALES)
         nc.sync.dma_start(offsets[:], offs)
-        load_up(3, 4)
-        load_scales(EARLY_TILES, ROW_TILES)
+        for a in range(1, PASSES):
+            down_raw[a] = load_pass(down, a, "down_raw")
+        for a in range(PASSES):
+            x_raw[a] = load_pass(x, a, "x_raw")
+        load_up(0)
+        load_codes(0, 2)
+        nc.sync.dma_start(out=weights[:, :HALF], in_=wgo[:, :HALF])
+        load_up(2)
         load_codes(2, 4)
-        load_up(4, 6)
+        nc.sync.dma_start(out=weights[:, HALF:], in_=wgo[:, HALF:])
+        load_scales(EARLY_SCALES, ROW_TILES)
+        load_up(4)
         load_codes(4, 8)
-        load_up(6, 8)
+        load_up(6)
 
         on_vector, on_scalar = nc.vector.tensor_copy, nc.scalar.copy
 
@@ -107,17 +113,22 @@ def tile_list_hscat_l_none_kernel(tc, x, w4_words, w4_scales, down, up, wgo, off
             )
             return grouped[:].rearrange("p c i -> p (c i)")
 
-        def quantize(flat, name):
-            width = flat.shape[1] // PACK
+        def operand(width, name):
             codes = keep.tile([P, width], U32, name=name + "_codes", align_bytes=64)
             scales = keep.tile([P, width], U8, name=name + "_scales", align_bytes=64)
-            nc.vector.quantize_mx(out=codes[:].bitcast(FP8X4), scales=scales[:], in_=flat)
             return codes, scales
 
-        down_q, x_q, up_q = {}, {}, {}
+        def quantize(flat, target, cols):
+            codes, scales = target
+            nc.vector.quantize_mx(out=codes[:, cols].bitcast(FP8X4), scales=scales[:, cols], in_=flat)
+
+        def columns(lo, hi):
+            return slice(lo * HALF, hi * HALF)
+
+        down_q, up_q = {}, {}
+        x_q = [operand(S, "x%d" % a) for a in range(PASSES)]
+        h_q = operand(S, "h")
         h_acc = [h_psum.tile([P, PACK, HALF], F32, name="h_acc%d" % half) for half in range(HALVES)]
-        h_codes = keep.tile([P, S], U32, name="h_codes", align_bytes=64)
-        h_scales = keep.tile([P, S], U8, name="h_scales", align_bytes=64)
 
         def quantize_down(a):
             flats = {}
@@ -129,22 +140,22 @@ def tile_list_hscat_l_none_kernel(tc, x, w4_words, w4_scales, down, up, wgo, off
                 )
                 flats[pair] = grouped[:].rearrange("p t m i -> p (t m i)")
             for pair in (1, 0):
-                down_q[a, pair] = quantize(flats[pair], "down%d_%d" % (a, pair))
+                down_q[a, pair] = operand(2 * P, "down%d_%d" % (a, pair))
+                quantize(flats[pair], down_q[a, pair], slice(0, 2 * P))
 
         def half_of_h(half, copy):
+            cols = columns(half, half + 1)
             for a in range(PASSES):
-                x_codes, x_scales = x_q[a, half] = quantize(
-                    interleave(copy, x_raw[a, half], "x_bf%d_%d" % (a, half)), "x%d_%d" % (a, half)
-                )
+                quantize(interleave(copy, x_raw[a][:, :, cols], "x_bf%d_%d" % (a, half)), x_q[a], cols)
                 for t in range(PACK):
                     d_codes, d_scales = down_q[a, t // 2]
-                    cols = slice((t % 2) * P, (t % 2 + 1) * P)
+                    m_cols = slice((t % 2) * P, (t % 2 + 1) * P)
                     nc.tensor.matmul_mx(
                         out=h_acc[half][:, t, :],
-                        lhsT=d_codes[:, cols].bitcast(FP8X4),
-                        lhsT_scale=d_scales[:, cols],
-                        rhs=x_codes[:].bitcast(FP8X4),
-                        rhs_scale=x_scales[:],
+                        lhsT=d_codes[:, m_cols].bitcast(FP8X4),
+                        lhsT_scale=d_scales[:, m_cols],
+                        rhs=x_q[a][0][:, cols].bitcast(FP8X4),
+                        rhs_scale=x_q[a][1][:, cols],
                         start=(a == 0 and t == 0),
                         stop=(a == PASSES - 1 and t == PACK - 1),
                     )
@@ -152,66 +163,58 @@ def tile_list_hscat_l_none_kernel(tc, x, w4_words, w4_scales, down, up, wgo, off
         def quantize_h(half):
             grouped = keep.tile([P, HALF, PACK], BF16, name="h_bf%d" % half, align_bytes=64)
             on_scalar(out=grouped[:], in_=h_acc[half][:].rearrange("p t j -> p j t"))
-            cols = slice(half * HALF, (half + 1) * HALF)
-            nc.vector.quantize_mx(
-                out=h_codes[:, cols].bitcast(FP8X4), scales=h_scales[:, cols], in_=grouped[:].rearrange("p j t -> p (j t)")
-            )
+            quantize(grouped[:].rearrange("p j t -> p (j t)"), h_q, columns(half, half + 1))
 
-        def quantize_up(n):
-            copy, run = (on_vector, LINE) if n < VECTOR_UP_TILES else (on_scalar, 1)
-            up_q[n] = quantize(interleave(copy, up_raw[n], "up_bf%d" % n, run), "up%d" % n)
+        def quantize_up(n, staging):
+            copy, run = (on_vector, LINE) if n < PAIR else (on_scalar, 1)
+            up_q[n] = operand(P, "up%d" % n)
+            quantize(interleave(copy, up_raw[n], staging, run), up_q[n], slice(0, P))
 
-        def product(n, lo, hi):
-            width = HALF * (hi - lo)
-            cols = slice(lo * HALF, hi * HALF)
-            acc = y_psum.tile([P, width], F32, name="y_acc")
-            for a in range(PASSES):
-                for half in range(lo, hi):
-                    x_codes, x_scales = x_q[a, half]
-                    nc.tensor.matmul_mx(
-                        out=acc[:, (half - lo) * HALF : (half - lo + 1) * HALF],
-                        lhsT=w4_code[n][:, a, :].bitcast(FP4X4),
-                        lhsT_scale=w4_scale[n][:, a, :],
-                        rhs=x_codes[:].bitcast(FP8X4),
-                        rhs_scale=x_scales[:],
-                        start=(a == 0 and half == lo),
-                        stop=False,
-                    )
-            nc.tensor.matmul_mx(
-                out=acc[:],
-                lhsT=up_q[n][0][:].bitcast(FP8X4),
-                lhsT_scale=up_q[n][1][:],
-                rhs=h_codes[:, cols].bitcast(FP8X4),
-                rhs_scale=h_scales[:, cols],
-                start=False,
-                stop=True,
-            )
-            y = keep.tile([P, width], F32, name="y%d_%d" % (n, lo))
-            on_scalar(out=y[:], in_=acc[:])
+        def product(n, lo, hi, y, up_first=False):
+            cols = columns(lo, hi)
+            acc = y_psum.tile([P, HALF * (hi - lo)], F32, name="y_acc")
+            w4_passes = [(w4_code[n][:, a, :].bitcast(FP4X4), w4_scale[n][:, a, :], x_q[a]) for a in range(PASSES)]
+            up_pass = [(up_q[n][0][:].bitcast(FP8X4), up_q[n][1][:], h_q)]
+            passes = up_pass + w4_passes if up_first else w4_passes + up_pass
+            for step, (lhs_codes, lhs_scales, (rhs_codes, rhs_scales)) in enumerate(passes):
+                nc.tensor.matmul_mx(
+                    out=acc[:],
+                    lhsT=lhs_codes,
+                    lhsT_scale=lhs_scales,
+                    rhs=rhs_codes[:, cols].bitcast(FP8X4),
+                    rhs_scale=rhs_scales[:, cols],
+                    start=(step == 0),
+                    stop=(step == len(passes) - 1),
+                )
+            on_scalar(out=y, in_=acc[:])
             nc.vector.tensor_tensor(
                 windows[n][:].indirect(offsets[:, cols.start // GROUP : cols.stop // GROUP]),
-                y[:],
+                y,
                 weights[:, cols],
                 mybir.AluOpType.mult,
             )
             if hi == HALVES:
                 nc.sync.dma_start(out=out[n * P : (n + 1) * P, :], in_=windows[n][:])
 
+        def staging(width, name):
+            return keep.tile([P, width], F32, name=name, align_bytes=64)[:]
+
         for a in range(PASSES):
             quantize_down(a)
         half_of_h(0, on_vector)
         quantize_h(0)
-        quantize_up(0)
-        product(0, 0, 1)
+        quantize_up(0, "up_bf0")
+        product(0, 0, 1, staging(HALF, "y_first"))
         half_of_h(1, on_scalar)
-        up_raw[2] = load_rows(up[:, 2 * P : 3 * P], "x_bf1_0", nc.scalar)[:]
-        quantize_up(1)
+        quantize_up(1, "h_bf0")
         quantize_h(1)
-        product(1, 0, 1)
-        product(0, 1, 2)
-        quantize_up(2)
-        product(1, 1, 2)
-        for n in range(EARLY_TILES, ROW_TILES):
-            if n + 1 < ROW_TILES:
-                quantize_up(n + 1)
-            product(n, 0, HALVES)
+        product(1, 0, 1, staging(HALF, "y_second"))
+        quantize_up(2, "up_bf2")
+        product(0, 1, 2, staging(HALF, "y_third"), up_first=True)
+        quantize_up(3, "up_bf3")
+        product(1, 1, 2, staging(HALF, "y_fourth"), up_first=True)
+        for n in range(PAIR, ROW_TILES - 1):
+            if n > PAIR:
+                quantize_up(n + 1, "up_bf%d" % (n + 1))
+            product(n, 0, HALVES, up_bytes[n + 1])
+        product(ROW_TILES - 1, 0, HALVES, staging(S, "y7"))

@@ -86,13 +86,13 @@ def tile_list_hscat_l_none_kernel(tc, x, w4_words, w4_scales, down, up, wgo, off
                 w4_scale[n] = scale_tile[lo][:, :, (n - lo) * P : (n - lo + 1) * P]
 
         down_raw[0] = load_pass(down, 0, "down_raw")
-        load_scales(0, EARLY_SCALES)
         nc.sync.dma_start(offsets[:], offs)
         for a in range(1, PASSES):
             down_raw[a] = load_pass(down, a, "down_raw")
         for a in range(PASSES):
             x_raw[a] = load_pass(x, a, "x_raw")
         load_up(0)
+        load_scales(0, EARLY_SCALES)
         load_codes(0, 2)
         nc.sync.dma_start(out=weights[:, :HALF], in_=wgo[:, :HALF])
         load_up(2)
@@ -206,9 +206,9 @@ def tile_list_hscat_l_none_kernel(tc, x, w4_words, w4_scales, down, up, wgo, off
         quantize_up(0, "up_bf0")
         product(0, 0, 1, staging(HALF, "y_first"))
         half_of_h(1, on_scalar)
-        quantize_up(1, "h_bf0")
+        quantize_up(1, "up_bf1")
         quantize_h(1)
-        product(1, 0, 1, staging(HALF, "y_second"))
+        product(1, 0, 1, staging(HALF, "y_second"), up_first=True)
         quantize_up(2, "up_bf2")
         product(0, 1, 2, staging(HALF, "y_third"), up_first=True)
         quantize_up(3, "up_bf3")

@@ -50,8 +50,8 @@ def tile_list_hscat_l_none_kernel(tc, x, w4_words, w4_scales, down, up, wgo, off
 
         down_raw, x_raw, up_raw, up_bytes, w4_code, w4_scale = {}, {}, {}, {}, {}, {}
 
-        def load_rows(rows, raw):
-            nc.sync.dma_start(out=raw, in_=rows.rearrange("(p i) c -> p i c", i=PACK))
+        def load_rows(rows, raw, queue=nc.sync):
+            queue.dma_start(out=raw, in_=rows.rearrange("(p i) c -> p i c", i=PACK))
 
         def load_pass(source, a, name):
             raw = keep.tile([P, PACK, source.shape[1]], F32, name="%s%d" % (name, a), align_bytes=64)
@@ -65,6 +65,12 @@ def tile_list_hscat_l_none_kernel(tc, x, w4_words, w4_scales, down, up, wgo, off
             load_rows(up[:, lo * P : (lo + PAIR) * P], raw)
             up_raw[lo], up_raw[lo + 1] = raw[:, :, :P], raw[:, :, P:]
             up_bytes[lo], up_bytes[lo + 1] = room[:, :S], room[:, loaded : loaded + S]
+
+        def load_up_tile(n, name, queue):
+            raw = keep.tile([P, PACK, P], F32, name=name, align_bytes=64)
+            load_rows(up[:, n * P : (n + 1) * P], raw[:], queue)
+            up_raw[n] = raw[:]
+            up_bytes[n] = raw[:].rearrange("p i c -> p (i c)")[:, :S]
 
         def load_codes(lo, hi):
             codes = keep.tile([P, PASSES, 2 * P * (hi - lo)], U8, name="w4_code%d" % lo, align_bytes=64)
@@ -85,19 +91,17 @@ def tile_list_hscat_l_none_kernel(tc, x, w4_words, w4_scales, down, up, wgo, off
             for n in range(lo, hi):
                 w4_scale[n] = scale_tile[lo][:, :, (n - lo) * P : (n - lo + 1) * P]
 
-        down_raw[0] = load_pass(down, 0, "down_raw")
-        nc.sync.dma_start(offsets[:], offs)
-        for a in range(1, PASSES):
+        for a in range(PASSES):
             down_raw[a] = load_pass(down, a, "down_raw")
         for a in range(PASSES):
             x_raw[a] = load_pass(x, a, "x_raw")
         load_up(0)
         load_scales(0, EARLY_SCALES)
         load_codes(0, 2)
-        nc.sync.dma_start(out=weights[:, :HALF], in_=wgo[:, :HALF])
-        load_up(2)
+        nc.sync.dma_start(out=weights[:], in_=wgo)
+        nc.sync.dma_start(offsets[:], offs)
+        load_up_tile(3, "up_raw3", nc.sync)
         load_codes(2, 4)
-        nc.sync.dma_start(out=weights[:, HALF:], in_=wgo[:, HALF:])
         load_scales(EARLY_SCALES, ROW_TILES)
         load_up(4)
         load_codes(4, 8)
@@ -166,7 +170,7 @@ def tile_list_hscat_l_none_kernel(tc, x, w4_words, w4_scales, down, up, wgo, off
             quantize(grouped[:].rearrange("p j t -> p (j t)"), h_q, columns(half, half + 1))
 
         def quantize_up(n, staging):
-            copy, run = (on_vector, LINE) if n < PAIR else (on_scalar, 1)
+            copy, run = (on_vector, LINE) if n <= PAIR else (on_scalar, 1)
             up_q[n] = operand(P, "up%d" % n)
             quantize(interleave(copy, up_raw[n], staging, run), up_q[n], slice(0, P))
 
@@ -206,15 +210,14 @@ def tile_list_hscat_l_none_kernel(tc, x, w4_words, w4_scales, down, up, wgo, off
         quantize_up(0, "up_bf0")
         product(0, 0, 1, staging(HALF, "y_first"))
         half_of_h(1, on_scalar)
+        load_up_tile(2, "x_bf1_0", nc.scalar)
         quantize_up(1, "up_bf1")
         quantize_h(1)
         product(1, 0, 1, staging(HALF, "y_second"), up_first=True)
-        quantize_up(2, "up_bf2")
         product(0, 1, 2, staging(HALF, "y_third"), up_first=True)
-        quantize_up(3, "up_bf3")
+        quantize_up(2, "up_bf2")
         product(1, 1, 2, staging(HALF, "y_fourth"), up_first=True)
         for n in range(PAIR, ROW_TILES - 1):
-            if n > PAIR:
-                quantize_up(n + 1, "up_bf%d" % (n + 1))
+            quantize_up(n + 1, "up_bf%d" % (n + 1))
             product(n, 0, HALVES, up_bytes[n + 1])
         product(ROW_TILES - 1, 0, HALVES, staging(S, "y7"))

@@ -129,6 +129,10 @@ def tile_list_hscat_l_none_kernel(tc, x, w4_words, w4_scales, down, up, wgo, off
         def columns(lo, hi):
             return slice(lo * HALF, hi * HALF)
 
+        def parts(cols):
+            middle = (cols.start + cols.stop) // 2
+            return slice(cols.start, middle), slice(middle, cols.stop)
+
         down_q, up_q = {}, {}
         x_q = [operand(S, "x%d" % a) for a in range(PASSES)]
         h_q = operand(S, "h")
@@ -150,7 +154,11 @@ def tile_list_hscat_l_none_kernel(tc, x, w4_words, w4_scales, down, up, wgo, off
         def half_of_h(half, copy):
             cols = columns(half, half + 1)
             for a in range(PASSES):
-                quantize(interleave(copy, x_raw[a][:, :, cols], "x_bf%d_%d" % (a, half)), x_q[a], cols)
+                if half == 0 and a == PASSES - 1:
+                    for part, part_copy in zip(parts(cols), (on_vector, on_scalar)):
+                        quantize(interleave(part_copy, x_raw[a][:, :, part], "x_last%d" % part.start), x_q[a], part)
+                else:
+                    quantize(interleave(copy, x_raw[a][:, :, cols], "x_bf%d_%d" % (a, half)), x_q[a], cols)
                 for t in range(PACK):
                     d_codes, d_scales = down_q[a, t // 2]
                     m_cols = slice((t % 2) * P, (t % 2 + 1) * P)
@@ -165,9 +173,13 @@ def tile_list_hscat_l_none_kernel(tc, x, w4_words, w4_scales, down, up, wgo, off
                     )
 
         def quantize_h(half):
-            grouped = keep.tile([P, HALF, PACK], BF16, name="h_bf%d" % half, align_bytes=64)
-            on_scalar(out=grouped[:], in_=h_acc[half][:].rearrange("p t j -> p j t"))
-            quantize(grouped[:].rearrange("p j t -> p (j t)"), h_q, columns(half, half + 1))
+            whole = slice(0, HALF)
+            for part in parts(whole) if half == 0 else (whole,):
+                width = part.stop - part.start
+                grouped = keep.tile([P, width, PACK], BF16, name="h_bf%d_%d" % (half, part.start), align_bytes=64)
+                on_scalar(out=grouped[:], in_=h_acc[half][:, :, part].rearrange("p t j -> p j t"))
+                cols = slice(half * HALF + part.start, half * HALF + part.stop)
+                quantize(grouped[:].rearrange("p j t -> p (j t)"), h_q, cols)
 
         def quantize_up(n, staging):
             copy, run = (on_vector, LINE) if n <= PAIR else (on_scalar, 1)

@@ -48,6 +48,7 @@ def tile_list_hscat_l_none_kernel(tc, x, w4_words, w4_scales, down, up, wgo, off
         for window in windows:
             nc.vector.memset(window[:], 0.0)
 
+        up_pair = {}
         down_raw, x_raw, up_raw, up_bytes, w4_code, w4_scale = {}, {}, {}, {}, {}, {}
 
         def load_rows(rows, raw, queue=nc.sync):
@@ -64,6 +65,7 @@ def tile_list_hscat_l_none_kernel(tc, x, w4_words, w4_scales, down, up, wgo, off
             raw = room[:, HALF : HALF + loaded].rearrange("p (i c) -> p i c", i=PACK)
             load_rows(up[:, lo * P : (lo + PAIR) * P], raw)
             up_raw[lo], up_raw[lo + 1] = raw[:, :, :P], raw[:, :, P:]
+            up_pair[lo] = raw
             up_bytes[lo], up_bytes[lo + 1] = room[:, :S], room[:, loaded : loaded + S]
 
         def load_up_tile(n, name, queue):
@@ -186,11 +188,17 @@ def tile_list_hscat_l_none_kernel(tc, x, w4_words, w4_scales, down, up, wgo, off
             up_q[n] = operand(P, "up%d" % n)
             quantize(interleave(copy, up_raw[n], staging, run), up_q[n], slice(0, P))
 
+        def quantize_up_pair(lo):
+            codes, scales = operand(PAIR * P, "up%d" % lo)
+            quantize(interleave(on_scalar, up_pair[lo], "up_bf%d" % lo, 1), (codes, scales), slice(0, PAIR * P))
+            for n in range(PAIR):
+                up_q[lo + n] = codes[:, n * P : (n + 1) * P], scales[:, n * P : (n + 1) * P]
+
         def product(n, lo, hi, y, up_first=False):
             cols = columns(lo, hi)
             acc = y_psum.tile([P, HALF * (hi - lo)], F32, name="y_acc")
             w4_passes = [(w4_code[n][:, a, :].bitcast(FP4X4), w4_scale[n][:, a, :], x_q[a]) for a in range(PASSES)]
-            up_pass = [(up_q[n][0][:].bitcast(FP8X4), up_q[n][1][:], h_q)]
+            up_pass = [(up_q[n][0][:, :].bitcast(FP8X4), up_q[n][1][:, :], h_q)]
             passes = up_pass + w4_passes if up_first else w4_passes + up_pass
             for step, (lhs_codes, lhs_scales, (rhs_codes, rhs_scales)) in enumerate(passes):
                 nc.tensor.matmul_mx(
@@ -230,6 +238,9 @@ def tile_list_hscat_l_none_kernel(tc, x, w4_words, w4_scales, down, up, wgo, off
         quantize_up(2, "up_bf2")
         product(1, 1, 2, staging(HALF, "y_fourth"), up_first=True)
         for n in range(PAIR, ROW_TILES - 1):
-            quantize_up(n + 1, "up_bf%d" % (n + 1))
+            if n + 1 in up_pair:
+                quantize_up_pair(n + 1)
+            elif n + 1 not in up_q:
+                quantize_up(n + 1, "up_bf%d" % (n + 1))
             product(n, 0, HALVES, up_bytes[n + 1])
         product(ROW_TILES - 1, 0, HALVES, staging(S, "y7"))

@@ -27,6 +27,7 @@ SCALE_ROWS = 4
 LINE = 4
 PAIR = 2
 EARLY_SCALES = 3
+WARM_PASSES = 3
 Y_BANKS = 6
 
 
@@ -225,6 +226,18 @@ def tile_list_hscat_l_none_kernel(tc, x, w4_words, w4_scales, down, up, wgo, off
 
         for a in range(PASSES):
             quantize_down(a)
+        warm = y_psum.tile([P, S], F32, name="y_acc")
+        warm_codes, warm_scales = down_q[PASSES - 1, 1]
+        for step in range(WARM_PASSES):
+            nc.tensor.matmul_mx(
+                out=warm[:],
+                lhsT=warm_codes[:, :P].bitcast(FP8X4),
+                lhsT_scale=warm_scales[:, :P],
+                rhs=warm_codes[:].bitcast(FP8X4),
+                rhs_scale=warm_scales[:],
+                start=True,
+                stop=True,
+            )
         half_of_h(0, on_vector)
         quantize_h(0)
         quantize_up(0, "up_bf0")

@@ -28,6 +28,7 @@ LINE = 4
 PAIR = 2
 EARLY_SCALES = 3
 WARM_PASSES = 3
+DMA_ALIGN = 256
 Y_BANKS = 6
 
 
@@ -38,13 +39,13 @@ def tile_list_hscat_l_none_kernel(tc, x, w4_words, w4_scales, down, up, wgo, off
         h_psum = ctx.enter_context(tc.psum_pool(name="h_psum", bufs=1))
         y_psum = ctx.enter_context(tc.psum_pool(name="y_psum", bufs=Y_BANKS))
 
-        offsets = keep.tile([P, S // GROUP], U16, name="offsets")
-        weights = keep.tile([P, S], F32, name="weights")
-        windows = [keep.tile([P, T], F32, name="window%d" % n) for n in range(ROW_TILES)]
+        offsets = keep.tile([P, S // GROUP], U16, name="offsets", align_bytes=DMA_ALIGN)
+        weights = keep.tile([P, S], F32, name="weights", align_bytes=DMA_ALIGN)
+        windows = [keep.tile([P, T], F32, name="window%d" % n, align_bytes=DMA_ALIGN) for n in range(ROW_TILES)]
 
         scale_tile = {}
         for lo, hi in ((0, EARLY_SCALES), (EARLY_SCALES, ROW_TILES)):
-            scale_tile[lo] = keep.tile([P, PASSES, P * (hi - lo)], U8, name="w4_scale%d" % lo, align_bytes=64)
+            scale_tile[lo] = keep.tile([P, PASSES, P * (hi - lo)], U8, name="w4_scale%d" % lo, align_bytes=DMA_ALIGN)
             nc.vector.memset(scale_tile[lo][:].rearrange("p a n -> p (a n)").bitcast(U32), 0)
         for window in windows:
             nc.vector.memset(window[:], 0.0)
@@ -56,13 +57,13 @@ def tile_list_hscat_l_none_kernel(tc, x, w4_words, w4_scales, down, up, wgo, off
             queue.dma_start(out=raw, in_=rows.rearrange("(p i) c -> p i c", i=PACK))
 
         def load_pass(source, a, name):
-            raw = keep.tile([P, PACK, source.shape[1]], F32, name="%s%d" % (name, a), align_bytes=64)
+            raw = keep.tile([P, PACK, source.shape[1]], F32, name="%s%d" % (name, a), align_bytes=DMA_ALIGN)
             load_rows(source[a * K_PASS : (a + 1) * K_PASS, :], raw[:])
             return raw
 
         def load_up(lo):
             loaded = PACK * PAIR * P
-            room = keep.tile([P, HALF + loaded + HALF], F32, name="up_room%d" % lo, align_bytes=64)
+            room = keep.tile([P, HALF + loaded + HALF], F32, name="up_room%d" % lo, align_bytes=DMA_ALIGN)
             raw = room[:, HALF : HALF + loaded].rearrange("p (i c) -> p i c", i=PACK)
             load_rows(up[:, lo * P : (lo + PAIR) * P], raw)
             up_raw[lo], up_raw[lo + 1] = raw[:, :, :P], raw[:, :, P:]
@@ -70,13 +71,13 @@ def tile_list_hscat_l_none_kernel(tc, x, w4_words, w4_scales, down, up, wgo, off
             up_bytes[lo], up_bytes[lo + 1] = room[:, :S], room[:, loaded : loaded + S]
 
         def load_up_tile(n, name, queue):
-            raw = keep.tile([P, PACK, P], F32, name=name, align_bytes=64)
+            raw = keep.tile([P, PACK, P], F32, name=name, align_bytes=DMA_ALIGN)
             load_rows(up[:, n * P : (n + 1) * P], raw[:], queue)
             up_raw[n] = raw[:]
             up_bytes[n] = raw[:].rearrange("p i c -> p (i c)")[:, :S]
 
         def load_codes(lo, hi):
-            codes = keep.tile([P, PASSES, 2 * P * (hi - lo)], U8, name="w4_code%d" % lo, align_bytes=64)
+            codes = keep.tile([P, PASSES, 2 * P * (hi - lo)], U8, name="w4_code%d" % lo, align_bytes=DMA_ALIGN)
             nc.sync.dma_start(
                 out=codes[:].bitcast(I32),
                 in_=w4_words[:, :, 2 * P * lo : 2 * P * hi].rearrange("a p n -> p a n").bitcast(I32),
@@ -113,7 +114,7 @@ def tile_list_hscat_l_none_kernel(tc, x, w4_words, w4_scales, down, up, wgo, off
         on_vector, on_scalar = nc.vector.tensor_copy, nc.scalar.copy
 
         def interleave(copy, raw_cols, name, run=LINE):
-            grouped = keep.tile([P, raw_cols.shape[2], PACK], BF16, name=name, align_bytes=64)
+            grouped = keep.tile([P, raw_cols.shape[2], PACK], BF16, name=name, align_bytes=DMA_ALIGN)
             copy(
                 out=grouped[:].rearrange("p (c e) i -> p c i e", e=run),
                 in_=raw_cols.rearrange("p i (c e) -> p c i e", e=run),
@@ -121,8 +122,8 @@ def tile_list_hscat_l_none_kernel(tc, x, w4_words, w4_scales, down, up, wgo, off
             return grouped[:].rearrange("p c i -> p (c i)")
 
         def operand(width, name):
-            codes = keep.tile([P, width], U32, name=name + "_codes", align_bytes=64)
-            scales = keep.tile([P, width], U8, name=name + "_scales", align_bytes=64)
+            codes = keep.tile([P, width], U32, name=name + "_codes", align_bytes=DMA_ALIGN)
+            scales = keep.tile([P, width], U8, name=name + "_scales", align_bytes=DMA_ALIGN)
             return codes, scales
 
         def quantize(flat, target, cols):
@@ -144,7 +145,7 @@ def tile_list_hscat_l_none_kernel(tc, x, w4_words, w4_scales, down, up, wgo, off
         def quantize_down(a):
             flats = {}
             for pair, copy in ((1, on_vector), (0, on_scalar)):
-                grouped = keep.tile([P, 2, P, PACK], BF16, name="down_bf%d_%d" % (a, pair), align_bytes=64)
+                grouped = keep.tile([P, 2, P, PACK], BF16, name="down_bf%d_%d" % (a, pair), align_bytes=DMA_ALIGN)
                 copy(
                     out=grouped[:].rearrange("p t m i -> p m i t"),
                     in_=down_raw[a][:].rearrange("p i (m t) -> p m i t", t=PACK)[:, :, :, 2 * pair : 2 * pair + 2],
@@ -179,7 +180,7 @@ def tile_list_hscat_l_none_kernel(tc, x, w4_words, w4_scales, down, up, wgo, off
             whole = slice(0, HALF)
             for part in parts(whole) if half == 0 else (whole,):
                 width = part.stop - part.start
-                grouped = keep.tile([P, width, PACK], BF16, name="h_bf%d_%d" % (half, part.start), align_bytes=64)
+                grouped = keep.tile([P, width, PACK], BF16, name="h_bf%d_%d" % (half, part.start), align_bytes=DMA_ALIGN)
                 on_scalar(out=grouped[:], in_=h_acc[half][:, :, part].rearrange("p t j -> p j t"))
                 cols = slice(half * HALF + part.start, half * HALF + part.stop)
                 quantize(grouped[:].rearrange("p j t -> p (j t)"), h_q, cols)
@@ -222,7 +223,7 @@ def tile_list_hscat_l_none_kernel(tc, x, w4_words, w4_scales, down, up, wgo, off
                 nc.sync.dma_start(out=out[n * P : (n + 1) * P, :], in_=windows[n][:])
 
         def staging(width, name):
-            return keep.tile([P, width], F32, name=name, align_bytes=64)[:]
+            return keep.tile([P, width], F32, name=name, align_bytes=DMA_ALIGN)[:]
 
         for a in range(PASSES):
             quantize_down(a)

@@ -157,9 +157,10 @@ def tile_list_hscat_l_none_kernel(tc, x, w4_words, w4_scales, down, up, wgo, off
 
         def half_of_h(half, copy):
             cols = columns(half, half + 1)
-            for a in range(PASSES):
+            order = range(PASSES) if half == 0 else (0, 2, 1)
+            for step, a in enumerate(order):
                 if half == 0 and a == PASSES - 1:
-                    for part, part_copy in zip(parts(cols), (on_vector, on_scalar)):
+                    for part, part_copy in zip(parts(cols), (on_vector, on_vector)):
                         quantize(interleave(part_copy, x_raw[a][:, :, part], "x_last%d" % part.start), x_q[a], part)
                 else:
                     quantize(interleave(copy, x_raw[a][:, :, cols], "x_bf%d_%d" % (a, half)), x_q[a], cols)
@@ -172,8 +173,8 @@ def tile_list_hscat_l_none_kernel(tc, x, w4_words, w4_scales, down, up, wgo, off
                         lhsT_scale=d_scales[:, m_cols],
                         rhs=x_q[a][0][:, cols].bitcast(FP8X4),
                         rhs_scale=x_q[a][1][:, cols],
-                        start=(a == 0 and t == 0),
-                        stop=(a == PASSES - 1 and t == PACK - 1),
+                        start=(step == 0 and t == 0),
+                        stop=(step == PASSES - 1 and t == PACK - 1),
                     )
 
         def quantize_h(half):
@@ -188,7 +189,10 @@ def tile_list_hscat_l_none_kernel(tc, x, w4_words, w4_scales, down, up, wgo, off
         def quantize_up(n, staging):
             copy, run = (on_vector, LINE) if n <= PAIR else (on_scalar, 1)
             up_q[n] = operand(P, "up%d" % n)
-            quantize(interleave(copy, up_raw[n], staging, run), up_q[n], slice(0, P))
+            whole = slice(0, P)
+            for part in parts(whole) if n == PAIR else (whole,):
+                flat = interleave(copy, up_raw[n][:, :, part], "%s_%d" % (staging, part.start), run)
+                quantize(flat, up_q[n], part)
 
         def quantize_up_pair(lo):
             codes, scales = operand(PAIR * P, "up%d" % lo)

@@ -26,7 +26,7 @@ QUADRANT = 32
 SCALE_ROWS = 4
 LINE = 4
 PAIR = 2
-EARLY_SCALES = 3
+EARLY_SCALES = 2
 WARM_PASSES = 3
 DMA_ALIGN = 256
 Y_BANKS = 6

@@ -36,12 +36,13 @@ def tile_list_hscat_l_none_kernel(tc, x, w4_words, w4_scales, down, up, wgo, off
     nc = tc.nc
     with ExitStack() as ctx:
         keep = ctx.enter_context(tc.tile_pool(name="keep", bufs=1))
+        far = ctx.enter_context(tc.tile_pool(name="far", bufs=1))
         h_psum = ctx.enter_context(tc.psum_pool(name="h_psum", bufs=1))
         y_psum = ctx.enter_context(tc.psum_pool(name="y_psum", bufs=Y_BANKS))
 
         offsets = keep.tile([P, S // GROUP], U16, name="offsets", align_bytes=DMA_ALIGN)
         weights = keep.tile([P, S], F32, name="weights", align_bytes=DMA_ALIGN)
-        windows = [keep.tile([P, T], F32, name="window%d" % n, align_bytes=DMA_ALIGN) for n in range(ROW_TILES)]
+        windows = [(keep, far)[n % 2].tile([P, T], F32, name="window%d" % n, align_bytes=DMA_ALIGN) for n in range(ROW_TILES)]
 
         scale_tile = {}
         for lo, hi in ((0, EARLY_SCALES), (EARLY_SCALES, ROW_TILES)):

@@ -27,7 +27,6 @@ SCALE_ROWS = 4
 LINE = 4
 PAIR = 2
 EARLY_SCALES = 2
-WARM_PASSES = 3
 DMA_ALIGN = 256
 Y_BANKS = 6
 
@@ -232,18 +231,6 @@ def tile_list_hscat_l_none_kernel(tc, x, w4_words, w4_scales, down, up, wgo, off
 
         for a in range(PASSES):
             quantize_down(a)
-        warm = y_psum.tile([P, S], F32, name="y_acc")
-        warm_codes, warm_scales = down_q[PASSES - 1, 1]
-        for step in range(WARM_PASSES):
-            nc.tensor.matmul_mx(
-                out=warm[:],
-                lhsT=warm_codes[:, :P].bitcast(FP8X4),
-                lhsT_scale=warm_scales[:, :P],
-                rhs=warm_codes[:].bitcast(FP8X4),
-                rhs_scale=warm_scales[:],
-                start=True,
-                stop=True,
-            )
         half_of_h(0, on_vector)
         quantize_h(0)
         quantize_up(0, "up_bf0")

from contextlib import ExitStack

import concourse.mybir as mybir

K, M, T, S, R = 1536, 1024, 512, 256, 512
FLOPS = 2 * S * (K * R + K * M + R * M)

F32 = mybir.dt.float32
BF16 = mybir.dt.bfloat16
I32 = mybir.dt.int32
U32 = mybir.dt.uint32
U16 = mybir.dt.uint16
U8 = mybir.dt.uint8
FP8X4 = mybir.dt.float8_e4m3fn_x4
FP4X4 = mybir.dt.float4_e2m1fn_x4

P = 128
PACK = 4
K_PASS = P * PACK
PASSES = K // K_PASS
HALF = 128
HALVES = S // HALF
ROW_TILES = M // P
GROUP = 16
QUADRANT = 32
SCALE_ROWS = 4
LINE = 4
PAIR = 2
EARLY_SCALES = 2
DMA_ALIGN = 256
Y_BANKS = 6


def tile_list_hscat_l_none_kernel(tc, x, w4_words, w4_scales, down, up, wgo, offs, out):
    nc = tc.nc
    with ExitStack() as ctx:
        keep = ctx.enter_context(tc.tile_pool(name="keep", bufs=1))
        far = ctx.enter_context(tc.tile_pool(name="far", bufs=1))
        h_psum = ctx.enter_context(tc.psum_pool(name="h_psum", bufs=1))
        y_psum = ctx.enter_context(tc.psum_pool(name="y_psum", bufs=Y_BANKS))

        offsets = keep.tile([P, S // GROUP], U16, name="offsets", align_bytes=DMA_ALIGN)
        weights = keep.tile([P, S], F32, name="weights", align_bytes=DMA_ALIGN)
        windows = [(keep, far)[n % 2].tile([P, T], F32, name="window%d" % n, align_bytes=DMA_ALIGN) for n in range(ROW_TILES)]

        scale_tile = {}
        for lo, hi in ((0, EARLY_SCALES), (EARLY_SCALES, ROW_TILES)):
            scale_tile[lo] = keep.tile([P, PASSES, P * (hi - lo)], U8, name="w4_scale%d" % lo, align_bytes=DMA_ALIGN)
            nc.vector.memset(scale_tile[lo][:].rearrange("p a n -> p (a n)").bitcast(U32), 0)
        for window in windows:
            nc.vector.memset(window[:], 0.0)

        up_pair = {}
        down_raw, x_raw, up_raw, up_bytes, w4_code, w4_scale = {}, {}, {}, {}, {}, {}

        def load_rows(rows, raw, queue=nc.sync):
            queue.dma_start(out=raw, in_=rows.rearrange("(p i) c -> p i c", i=PACK))

        def load_pass(source, a, name):
            raw = keep.tile([P, PACK, source.shape[1]], F32, name="%s%d" % (name, a), align_bytes=DMA_ALIGN)
            load_rows(source[a * K_PASS : (a + 1) * K_PASS, :], raw[:])
            return raw

        def load_up(lo):
            loaded = PACK * PAIR * P
            room = keep.tile([P, HALF + loaded + HALF], F32, name="up_room%d" % lo, align_bytes=DMA_ALIGN)
            raw = room[:, HALF : HALF + loaded].rearrange("p (i c) -> p i c", i=PACK)
            load_rows(up[:, lo * P : (lo + PAIR) * P], raw)
            up_raw[lo], up_raw[lo + 1] = raw[:, :, :P], raw[:, :, P:]
            up_pair[lo] = raw
            up_bytes[lo], up_bytes[lo + 1] = room[:, :S], room[:, loaded : loaded + S]

        def load_up_tile(n, name, queue):
            raw = keep.tile([P, PACK, P], F32, name=name, align_bytes=DMA_ALIGN)
            load_rows(up[:, n * P : (n + 1) * P], raw[:], queue)
            up_raw[n] = raw[:]
            up_bytes[n] = raw[:].rearrange("p i c -> p (i c)")[:, :S]

        def load_codes(lo, hi):
            codes = keep.tile([P, PASSES, 2 * P * (hi - lo)], U8, name="w4_code%d" % lo, align_bytes=DMA_ALIGN)
            nc.sync.dma_start(
                out=codes[:].bitcast(I32),
                in_=w4_words[:, :, 2 * P * lo : 2 * P * hi].rearrange("a p n -> p a n").bitcast(I32),
            )
            for n in range(lo, hi):
                w4_code[n] = codes[:, :, (n - lo) * 2 * P : (n - lo + 1) * 2 * P]

        def load_scales(lo, hi):
            for row in range(SCALE_ROWS):
                rows = w4_scales[:, row::SCALE_ROWS, P * lo : P * hi]
                nc.sync.dma_start(
                    out=scale_tile[lo][row:P:QUADRANT, :, :].bitcast(I32),
                    in_=rows.rearrange("a q n -> q a n").bitcast(I32),
                )
            for n in range(lo, hi):
                w4_scale[n] = scale_tile[lo][:, :, (n - lo) * P : (n - lo + 1) * P]

        for a in range(PASSES):
            down_raw[a] = load_pass(down, a, "down_raw")
        for a in range(PASSES):
            x_raw[a] = load_pass(x, a, "x_raw")
        load_up(0)
        load_scales(0, EARLY_SCALES)
        load_codes(0, 2)
        nc.sync.dma_start(out=weights[:], in_=wgo)
        nc.sync.dma_start(offsets[:], offs)
        load_up_tile(3, "up_raw3", nc.sync)
        load_codes(2, 4)
        load_scales(EARLY_SCALES, ROW_TILES)
        load_up(4)
        load_codes(4, 8)
        load_up(6)

        on_vector, on_scalar = nc.vector.tensor_copy, nc.scalar.copy

        def interleave(copy, raw_cols, name, run=LINE):
            grouped = keep.tile([P, raw_cols.shape[2], PACK], BF16, name=name, align_bytes=DMA_ALIGN)
            copy(
                out=grouped[:].rearrange("p (c e) i -> p c i e", e=run),
                in_=raw_cols.rearrange("p i (c e) -> p c i e", e=run),
            )
            return grouped[:].rearrange("p c i -> p (c i)")

        def operand(width, name):
            codes = keep.tile([P, width], U32, name=name + "_codes", align_bytes=DMA_ALIGN)
            scales = keep.tile([P, width], U8, name=name + "_scales", align_bytes=DMA_ALIGN)
            return codes, scales

        def quantize(flat, target, cols):
            codes, scales = target
            nc.vector.quantize_mx(out=codes[:, cols].bitcast(FP8X4), scales=scales[:, cols], in_=flat)

        def columns(lo, hi):
            return slice(lo * HALF, hi * HALF)

        def parts(cols):
            middle = (cols.start + cols.stop) // 2
            return slice(cols.start, middle), slice(middle, cols.stop)

        down_q, up_q = {}, {}
        x_q = [operand(S, "x%d" % a) for a in range(PASSES)]
        h_q = operand(S, "h")
        h_acc = [h_psum.tile([P, PACK, HALF], F32, name="h_acc%d" % half) for half in range(HALVES)]

        def quantize_down(a):
            flats = {}
            for pair, copy in ((1, on_vector), (0, on_scalar)):
                grouped = keep.tile([P, 2, P, PACK], BF16, name="down_bf%d_%d" % (a, pair), align_bytes=DMA_ALIGN)
                copy(
                    out=grouped[:].rearrange("p t m i -> p m i t"),
                    in_=down_raw[a][:].rearrange("p i (m t) -> p m i t", t=PACK)[:, :, :, 2 * pair : 2 * pair + 2],
                )
                flats[pair] = grouped[:].rearrange("p t m i -> p (t m i)")
            for pair in (1, 0):
                down_q[a, pair] = operand(2 * P, "down%d_%d" % (a, pair))
                quantize(flats[pair], down_q[a, pair], slice(0, 2 * P))

        def half_of_h(half, copy):
            cols = columns(half, half + 1)
            order = range(PASSES) if half == 0 else (0, 2, 1)
            for step, a in enumerate(order):
                if half == 0 and a == PASSES - 1:
                    for part, part_copy in zip(parts(cols), (on_vector, on_vector)):
                        quantize(interleave(part_copy, x_raw[a][:, :, part], "x_last%d" % part.start), x_q[a], part)
                else:
                    quantize(interleave(copy, x_raw[a][:, :, cols], "x_bf%d_%d" % (a, half)), x_q[a], cols)
                for t in range(PACK):
                    d_codes, d_scales = down_q[a, t // 2]
                    m_cols = slice((t % 2) * P, (t % 2 + 1) * P)
                    nc.tensor.matmul_mx(
                        out=h_acc[half][:, t, :],
                        lhsT=d_codes[:, m_cols].bitcast(FP8X4),
                        lhsT_scale=d_scales[:, m_cols],
                        rhs=x_q[a][0][:, cols].bitcast(FP8X4),
                        rhs_scale=x_q[a][1][:, cols],
                        start=(step == 0 and t == 0),
                        stop=(step == PASSES - 1 and t == PACK - 1),
                    )

        def quantize_h(half):
            whole = slice(0, HALF)
            for part in parts(whole) if half == 0 else (whole,):
                width = part.stop - part.start
                grouped = keep.tile([P, width, PACK], BF16, name="h_bf%d_%d" % (half, part.start), align_bytes=DMA_ALIGN)
                on_scalar(out=grouped[:], in_=h_acc[half][:, :, part].rearrange("p t j -> p j t"))
                cols = slice(half * HALF + part.start, half * HALF + part.stop)
                quantize(grouped[:].rearrange("p j t -> p (j t)"), h_q, cols)

        def quantize_up(n, staging):
            copy, run = (on_vector, LINE) if n <= PAIR else (on_scalar, 1)
            up_q[n] = operand(P, "up%d" % n)
            whole = slice(0, P)
            for part in parts(whole) if n == PAIR else (whole,):
                flat = interleave(copy, up_raw[n][:, :, part], "%s_%d" % (staging, part.start), run)
                quantize(flat, up_q[n], part)

        def quantize_up_pair(lo):
            codes, scales = operand(PAIR * P, "up%d" % lo)
            quantize(interleave(on_scalar, up_pair[lo], "up_bf%d" % lo, 1), (codes, scales), slice(0, PAIR * P))
            for n in range(PAIR):
                up_q[lo + n] = codes[:, n * P : (n + 1) * P], scales[:, n * P : (n + 1) * P]

        def product(n, lo, hi, y, up_first=False):
            cols = columns(lo, hi)
            acc = y_psum.tile([P, HALF * (hi - lo)], F32, name="y_acc")
            w4_passes = [(w4_code[n][:, a, :].bitcast(FP4X4), w4_scale[n][:, a, :], x_q[a]) for a in range(PASSES)]
            up_pass = [(up_q[n][0][:, :].bitcast(FP8X4), up_q[n][1][:, :], h_q)]
            passes = up_pass + w4_passes if up_first else w4_passes + up_pass
            for step, (lhs_codes, lhs_scales, (rhs_codes, rhs_scales)) in enumerate(passes):
                nc.tensor.matmul_mx(
                    out=acc[:],
                    lhsT=lhs_codes,
                    lhsT_scale=lhs_scales,
                    rhs=rhs_codes[:, cols].bitcast(FP8X4),
                    rhs_scale=rhs_scales[:, cols],
                    start=(step == 0),
                    stop=(step == len(passes) - 1),
                )
            on_scalar(out=y, in_=acc[:])
            nc.vector.tensor_tensor(
                windows[n][:].indirect(offsets[:, cols.start // GROUP : cols.stop // GROUP]),
                y,
                weights[:, cols],
                mybir.AluOpType.mult,
            )
            if hi == HALVES:
                nc.sync.dma_start(out=out[n * P : (n + 1) * P, :], in_=windows[n][:])

        def staging(width, name):
            return keep.tile([P, width], F32, name=name, align_bytes=DMA_ALIGN)[:]

        for a in range(PASSES):
            quantize_down(a)
        half_of_h(0, on_vector)
        quantize_h(0)
        quantize_up(0, "up_bf0")
        product(0, 0, 1, staging(HALF, "y_first"))
        half_of_h(1, on_scalar)
        load_up_tile(2, "x_bf1_0", nc.scalar)
        quantize_up(1, "up_bf1")
        quantize_h(1)
        product(1, 0, 1, staging(HALF, "y_second"), up_first=True)
        product(0, 1, 2, staging(HALF, "y_third"), up_first=True)
        quantize_up(2, "up_bf2")
        product(1, 1, 2, staging(HALF, "y_fourth"), up_first=True)
        for n in range(PAIR, ROW_TILES - 1):
            if n + 1 in up_pair:
                quantize_up_pair(n + 1)
            elif n + 1 not in up_q:
                quantize_up(n + 1, "up_bf%d" % (n + 1))
            product(n, 0, HALVES, up_bytes[n + 1])
        product(ROW_TILES - 1, 0, HALVES, staging(S, "y7"))
